import numpy as np
import ml_dtypes


def mxq(x, axis, fmt="e4m3"):
    dtype, down = {"e4m3": (ml_dtypes.float8_e4m3fn, 7), "e5m2": (ml_dtypes.float8_e5m2, 14)}[fmt]
    v = np.moveaxis(np.asarray(x, np.float32).astype(ml_dtypes.bfloat16).astype(np.float64), axis, -1)
    blocks = v.reshape(v.shape[:-1] + (-1, 32))
    amax = np.abs(blocks).max(-1, keepdims=True)
    byte = np.maximum(np.where(amax > 0, np.frexp(amax)[1] - 1 + 127, 0) - down, 1)
    scale = np.exp2(byte - 127.0)
    codes = (blocks / scale).astype(np.float32).astype(dtype).astype(np.float64)
    return np.moveaxis((codes * scale).reshape(v.shape), -1, axis)


WIDE = False


def mx_kscale(k):
    if not WIDE:
        return np.ones(k)
    levels = np.array([10, -10, 5, -5, 0])
    if k % 512:
        return np.exp2(np.random.permutation(np.resize(levels, k // 32))).repeat(32)
    a = np.empty((k // 512, 16))
    for p in range(k // 512):
        a[p, :8] = np.random.permutation(np.resize(levels, 8))
        for g in range(8):
            far = levels[np.abs(levels - a[p, g]) >= 10]
            a[p, g + 8] = far[np.random.randint(len(far))]
    return np.exp2(a.ravel()).repeat(32)


def f64(x):
    return np.asarray(x).astype(np.float64)


def striped(idx):
    return np.tile(idx.reshape(-1, 16).T, (8, 1)).astype(np.uint16)


def unstriped(offs):
    return offs[:16].T.reshape(-1).astype(np.int64)


def pack_weight(w):
    k, n = w.shape
    w = f64(np.asarray(w, np.float32).astype(ml_dtypes.bfloat16)).reshape(k // 32, 32, n)
    amax = np.abs(w).max(1)
    byte = np.clip(np.where(amax > 0, np.frexp(amax)[1] - 1 + 127 - 7, 1), 1, 254)
    scaled = (w * np.exp2(127.0 - byte)[:, None, :]).reshape(k, n).astype(np.float32)
    words = np.ascontiguousarray(scaled.reshape(k // 512, 128, 4, n).transpose(0, 1, 3, 2)).astype(ml_dtypes.float8_e4m3fn).view(np.uint8)
    return words, np.ascontiguousarray(byte.astype(np.uint8).reshape(k // 512, 16, n))


def unpack_weight(words, scales):
    g, p, n, _ = words.shape
    vals = np.ascontiguousarray(words).view(ml_dtypes.float8_e4m3fn).astype(np.float64) * np.repeat(np.exp2(scales.astype(np.float64) - 127.0), 8, axis=1)[..., None]
    return vals.transpose(0, 1, 3, 2).reshape(g * 512, n)


def planes(y):
    n, m = y.shape
    v = y.astype(np.float32).astype(ml_dtypes.bfloat16).astype(np.float64).reshape(n // 32, 32, m)
    top = np.abs(v).max(1)
    byte = np.clip(np.where(top > 0, np.frexp(top)[1] - 1 + 127 - 7, 1), 1, 254)
    codes = (v * np.exp2(127.0 - byte)[:, None, :]).reshape(n, m).astype(np.float32).astype(ml_dtypes.float8_e4m3fn).view(np.uint8)
    words = codes.reshape(n // 512, 128, 4, m).transpose(0, 1, 3, 2)
    return np.ascontiguousarray(words), np.ascontiguousarray(byte.astype(np.uint8).reshape(n // 512, 16, m))


def relu(v):
    return np.maximum(v, 0.0)


K, T, S, H, N, U = 512, 2048, 512, 512, 512, 1024


def setup_inputs():
    n = np.random.standard_normal
    s = mx_kscale(K)[:, None]
    u = mx_kscale(H)
    packed_xT = pack_weight(n((K, T)) * s)
    return {
        "x_words": packed_xT[0],
        "x_scales": packed_xT[1],
        "mem": (n((H, U)) * u[:, None]).astype(np.float32),
        "w1": (n((K, N)) / np.sqrt(2 * K) / s).astype(np.float32),
        "sr": (n((H, N)) / np.sqrt(2 * H) / u[:, None]).astype(np.float32),
        "thr": (-np.random.uniform(0.2, 0.8, (N, 1))).astype(np.float32),
        "offs": striped(np.random.permutation(T)[:S]),
        "slot": striped(np.random.permutation(U)[:S]),
    }


def reference(x_words, x_scales, mem, w1, sr, thr, offs, slot):
    h = f64(mem)[:, unstriped(slot)]
    xq = unpack_weight(x_words, x_scales)[:, unstriped(offs)]
    y = mxq(f64(sr), 0, "e4m3").T @ mxq(h, 0, "e4m3") + mxq(f64(w1), 0, "e4m3").T @ xq
    out_0 = relu(y + f64(thr)) - (relu(-1.0 * y + f64(thr)))
    return (out_0,) + planes(out_0)

@@ -1,0 +1,176 @@
+from contextlib import ExitStack
+
+import concourse.mybir as mybir
+
+K, T, S, H, N, U = 512, 2048, 512, 512, 512, 1024
+FLOPS = 2 * N * S * (K + H)
+
+F32 = mybir.dt.float32
+BF16 = mybir.dt.bfloat16
+I32 = mybir.dt.int32
+U32 = mybir.dt.uint32
+U16 = mybir.dt.uint16
+U8 = mybir.dt.uint8
+FP8X4 = mybir.dt.float8_e4m3fn_x4
+ALU = mybir.AluOpType
+ACT = mybir.ActivationFunctionType
+
+P = 128
+PACK = 4
+HALF = S // 2
+W_SPLIT = 56
+VECTOR_ALONE = {(1, 3)}
+
+
+def tile_picked_ylista_soft_po_kernel(
+    tc, x_words, x_scales, mem, w1, sr, thr, offs, slot, out_0, out_1, out_2
+):
+    nc = tc.nc
+    with ExitStack() as ctx:
+        keep = ctx.enter_context(tc.tile_pool(name="keep", bufs=1))
+        psum = ctx.enter_context(tc.psum_pool(name="psum", bufs=1))
+
+        slot_t = keep.tile([P, S // 16], U16, name="slot_t")
+        offs_t = keep.tile([P, S // 16], U16, name="offs_t")
+        thr_t = keep.tile([P, PACK], F32, name="thr_t")
+        neg_thr = keep.tile([P, PACK], F32, name="neg_thr")
+        mem_t = [keep.tile([P, U], F32, name=f"mem{j}") for j in range(PACK)]
+        sr_raw = keep.tile([P, PACK, N], F32, name="sr_raw")
+        w1_raw = keep.tile([P, PACK, N], F32, name="w1_raw")
+        xw_all = keep.tile([P, T], I32, name="xw_all")
+        xs_all = keep.tile([P, T], U8, name="xs_all")
+
+        nc.vector.memset(xs_all[:].bitcast(I32), 0)
+        nc.sync.dma_start(slot_t[:], slot)
+        mem_rows = mem.rearrange("(p j) u -> p j u", j=PACK)
+        for j in range(PACK):
+            nc.sync.dma_start(out=mem_t[j][:], in_=mem_rows[:, j, :])
+        nc.sync.dma_start(offs_t[:], offs)
+        for q in range(4):
+            nc.sync.dma_start(
+                out=xs_all[32 * q : 32 * q + 4, :].bitcast(I32),
+                in_=x_scales[0, 4 * q : 4 * q + 4, :].bitcast(I32),
+            )
+        nc.sync.dma_start(out=sr_raw[:], in_=sr.rearrange("(p j) c -> p j c", j=PACK))
+        nc.sync.dma_start(out=w1_raw[:], in_=w1.rearrange("(p j) c -> p j c", j=PACK))
+        nc.sync.dma_start(out=thr_t[:], in_=thr.rearrange("(p t) o -> p (t o)", t=PACK))
+        nc.sync.dma_start(out=xw_all[:], in_=x_words[0].rearrange("p n t -> p (n t)").bitcast(I32))
+
+        h_rows = keep.tile([P, PACK, S], F32, name="h_rows")
+        for j in range(PACK):
+            nc.vector.tensor_copy(h_rows[:, j, :], mem_t[j][:].indirect(slot_t[:]))
+        hs_bf = keep.tile([P, PACK * (S + N)], BF16, name="hs_bf", align_bytes=64)
+        nc.scalar.copy(
+            out=hs_bf[:, : PACK * S].rearrange("p (c i t) -> p c t i", i=4, t=PACK),
+            in_=h_rows[:].rearrange("p t (c i) -> p c t i", i=4),
+        )
+        xs_g = keep.tile([P, S], U8, name="xs_g", align_bytes=64)
+        nc.vector.tensor_copy(xs_g[:], xs_all[:].indirect(offs_t[:]))
+
+        def deal(dealt, raw, split):
+            dst = dealt.rearrange("p (t m j) -> p m j t", t=PACK, j=PACK)
+            src = raw[:].rearrange("p j (m t) -> p m j t", t=PACK)
+            if split < P:
+                nc.scalar.copy(out=dst[:, split:, :, :], in_=src[:, split:, :, :])
+            nc.vector.tensor_copy(out=dst[:, :split, :, :], in_=src[:, :split, :, :])
+
+        deal(hs_bf[:, PACK * S :], sr_raw, P)
+        hs_codes = keep.tile([P, S + N], U32, name="hs_codes", align_bytes=64)
+        hs_scales = keep.tile([P, S + N], U8, name="hs_scales", align_bytes=64)
+        nc.vector.quantize_mx(out=hs_codes[:].bitcast(FP8X4), scales=hs_scales[:], in_=hs_bf[:])
+        h_codes, h_scales = hs_codes[:, :S], hs_scales[:, :S]
+        sr_codes, sr_scales = hs_codes[:, S:], hs_scales[:, S:]
+
+        acc = {}
+        for half in range(2):
+            cols = slice(half * HALF, (half + 1) * HALF)
+            for t in range(PACK):
+                rows = slice(t * P, (t + 1) * P)
+                acc[half, t] = psum.tile([P, HALF], F32, name=f"acc{half}{t}")
+                nc.tensor.matmul_mx(out=acc[half, t][:], lhsT=sr_codes[:, rows].bitcast(FP8X4),
+                                    lhsT_scale=sr_scales[:, rows], rhs=h_codes[:, cols].bitcast(FP8X4),
+                                    rhs_scale=h_scales[:, cols], start=True, stop=False)
+        w1_bf = keep.tile([P, PACK * N], BF16, name="w1_bf", align_bytes=64)
+        deal(w1_bf[:], w1_raw, W_SPLIT)
+        w1_codes = keep.tile([P, N], U32, name="w1_codes", align_bytes=64)
+        w1_scales = keep.tile([P, N], U8, name="w1_scales", align_bytes=64)
+        nc.vector.quantize_mx(out=w1_codes[:].bitcast(FP8X4), scales=w1_scales[:], in_=w1_bf[:])
+
+        nc.scalar.activation(out=neg_thr[:], in_=thr_t[:], func=ACT.Copy, scale=-1.0)
+        xw_g = []
+        for half in range(2):
+            g = keep.tile([P, HALF], U32, name=f"xw_g{half}", align_bytes=64)
+            nc.vector.tensor_copy(g[:], xw_all[:].bitcast(U32).indirect(offs_t[:, half * (HALF // 16) : (half + 1) * (HALF // 16)]))
+            xw_g.append(g)
+        for half in range(2):
+            cols = slice(half * HALF, (half + 1) * HALF)
+            for t in range(PACK):
+                rows = slice(t * P, (t + 1) * P)
+                nc.tensor.matmul_mx(out=acc[half, t][:], lhsT=w1_codes[:, rows].bitcast(FP8X4),
+                                    lhsT_scale=w1_scales[:, rows], rhs=xw_g[half][:].bitcast(FP8X4),
+                                    rhs_scale=xs_g[:, cols], start=False, stop=True)
+
+        out_rows = out_0.rearrange("(p t) j -> p t j", t=PACK)
+        out_words = out_1[0].rearrange("p n t -> p (n t)").bitcast(I32)
+        y = [keep.tile([P, PACK, HALF], F32, name=f"y{half}") for half in range(2)]
+        up = [keep.tile([P, PACK, HALF], F32, name=f"up{half}") for half in range(2)]
+        down = [keep.tile([P, PACK, HALF], F32, name=f"down{half}") for half in range(2)]
+        y_bf = keep.tile([P, S, PACK], BF16, name="y_bf", align_bytes=64)
+        y_codes = keep.tile([P, S], U32, name="y_codes", align_bytes=64)
+        y_scales = keep.tile([P, S], U8, name="y_scales", align_bytes=64)
+
+        def relus(half, t):
+            a = acc[half, t]
+            nc.scalar.activation(out=up[half][:, t, :], in_=a[:], func=ACT.Relu, bias=thr_t[:, t : t + 1], scale=1.0)
+            nc.scalar.activation(out=down[half][:, t, :], in_=a[:], func=ACT.Relu, bias=thr_t[:, t : t + 1], scale=-1.0)
+
+        def sub(half, t0, t1):
+            nc.vector.tensor_tensor(y[half][:, t0:t1, :], up[half][:, t0:t1, :], down[half][:, t0:t1, :], ALU.subtract)
+
+        def alone(half, t):
+            a = acc[half, t]
+            nc.vector.tensor_scalar(out=up[half][:, t, :], in0=a[:], scalar1=neg_thr[:, t : t + 1], scalar2=None, op0=ALU.max)
+            nc.vector.scalar_tensor_tensor(out=y[half][:, t, :], in0=a[:], scalar=thr_t[:, t : t + 1], in1=up[half][:, t, :],
+                                           op0=ALU.min, op1=ALU.add)
+
+        def store(half, t0, t1):
+            nc.sync.dma_start(out=out_rows[:, t0:t1, half * HALF : (half + 1) * HALF], in_=y[half][:, t0:t1, :])
+
+        def cast(eng, half, c0, c1):
+            dst = y_bf[:, half * HALF + c0 : half * HALF + c1, :].rearrange("p (c i) t -> p c t i", i=4)
+            src = y[half][:, :, c0:c1].rearrange("p t (c i) -> p c t i", i=4)
+            if eng == "v":
+                nc.vector.tensor_copy(out=dst, in_=src)
+            else:
+                nc.scalar.copy(out=dst, in_=src)
+
+        def quant(c0, c1):
+            nc.vector.quantize_mx(out=y_codes[:, c0:c1].bitcast(FP8X4), scales=y_scales[:, c0:c1],
+                                  in_=y_bf[:, c0:c1, :].rearrange("p c t -> p (c t)"))
+            nc.sync.dma_start(out=out_words[:, c0:c1], in_=y_codes[:, c0:c1].bitcast(I32))
+
+        relus(0, 0)
+        alone(0, 1)
+        relus(0, 2)
+        relus(0, 3)
+        sub(0, 0, 1)
+        store(0, 0, 2)
+        alone(1, 0)
+        relus(1, 1)
+        sub(0, 2, 4)
+        store(0, 2, 4)
+        relus(1, 2)
+        relus(1, 3)
+        cast("v", 0, 176, 256)
+        sub(1, 1, 2)
+        store(1, 0, 2)
+        cast("s", 0, 0, 176)
+        sub(1, 2, 4)
+        store(1, 2, 4)
+        cast("v", 1, 0, 256)
+        quant(0, 256)
+        quant(256, 512)
+        for q in range(4):
+            eng = nc.scalar if q % 2 == 0 else nc.sync
+            eng.dma_start(out=out_2[0, 4 * q : 4 * q + 4, :].bitcast(I32),
+                          in_=y_scales[32 * q : 32 * q + 4, :].bitcast(I32))

@@ -18,7 +18,8 @@ ACT = mybir.ActivationFunctionType
 P = 128
 PACK = 4
 HALF = S // 2
-W_SPLIT = 56
+W_SPLIT = 48
+SR_SPLIT = 96
 VECTOR_ALONE = {(1, 3)}
 
 
@@ -47,7 +48,7 @@ def tile_picked_ylista_soft_po_kernel(
             nc.sync.dma_start(out=mem_t[j][:], in_=mem_rows[:, j, :])
         nc.sync.dma_start(offs_t[:], offs)
         for q in range(4):
-            nc.sync.dma_start(
+            nc.gpsimd.dma_start(
                 out=xs_all[32 * q : 32 * q + 4, :].bitcast(I32),
                 in_=x_scales[0, 4 * q : 4 * q + 4, :].bitcast(I32),
             )
@@ -57,13 +58,17 @@ def tile_picked_ylista_soft_po_kernel(
         nc.sync.dma_start(out=xw_all[:], in_=x_words[0].rearrange("p n t -> p (n t)").bitcast(I32))
 
         h_rows = keep.tile([P, PACK, S], F32, name="h_rows")
-        for j in range(PACK):
+        for j in range(PACK - 1):
             nc.vector.tensor_copy(h_rows[:, j, :], mem_t[j][:].indirect(slot_t[:]))
         hs_bf = keep.tile([P, PACK * (S + N)], BF16, name="hs_bf", align_bytes=64)
-        nc.scalar.copy(
-            out=hs_bf[:, : PACK * S].rearrange("p (c i t) -> p c t i", i=4, t=PACK),
-            in_=h_rows[:].rearrange("p t (c i) -> p c t i", i=4),
-        )
+        for half in range(2):
+            cols = slice(half * HALF, (half + 1) * HALF)
+            nc.vector.tensor_copy(h_rows[:, PACK - 1, cols],
+                                  mem_t[PACK - 1][:].indirect(slot_t[:, half * (HALF // 16) : (half + 1) * (HALF // 16)]))
+            nc.scalar.copy(
+                out=hs_bf[:, PACK * half * HALF : PACK * (half + 1) * HALF].rearrange("p (c i t) -> p c t i", i=4, t=PACK),
+                in_=h_rows[:, :, cols].rearrange("p t (c i) -> p c t i", i=4),
+            )
         xs_g = keep.tile([P, S], U8, name="xs_g", align_bytes=64)
         nc.vector.tensor_copy(xs_g[:], xs_all[:].indirect(offs_t[:]))
 
@@ -74,7 +79,7 @@ def tile_picked_ylista_soft_po_kernel(
                 nc.scalar.copy(out=dst[:, split:, :, :], in_=src[:, split:, :, :])
             nc.vector.tensor_copy(out=dst[:, :split, :, :], in_=src[:, :split, :, :])
 
-        deal(hs_bf[:, PACK * S :], sr_raw, P)
+        deal(hs_bf[:, PACK * S :], sr_raw, SR_SPLIT)
         hs_codes = keep.tile([P, S + N], U32, name="hs_codes", align_bytes=64)
         hs_scales = keep.tile([P, S + N], U8, name="hs_scales", align_bytes=64)
         nc.vector.quantize_mx(out=hs_codes[:].bitcast(FP8X4), scales=hs_scales[:], in_=hs_bf[:])
@@ -127,9 +132,12 @@ def tile_picked_ylista_soft_po_kernel(
         def sub(half, t0, t1):
             nc.vector.tensor_tensor(y[half][:, t0:t1, :], up[half][:, t0:t1, :], down[half][:, t0:t1, :], ALU.subtract)
 
-        def alone(half, t):
+        def upper(half, t):
             a = acc[half, t]
             nc.vector.tensor_scalar(out=up[half][:, t, :], in0=a[:], scalar1=neg_thr[:, t : t + 1], scalar2=None, op0=ALU.max)
+
+        def both(half, t):
+            a = acc[half, t]
             nc.vector.scalar_tensor_tensor(out=y[half][:, t, :], in0=a[:], scalar=thr_t[:, t : t + 1], in1=up[half][:, t, :],
                                            op0=ALU.min, op1=ALU.add)
 
@@ -150,25 +158,29 @@ def tile_picked_ylista_soft_po_kernel(
             nc.sync.dma_start(out=out_words[:, c0:c1], in_=y_codes[:, c0:c1].bitcast(I32))
 
         relus(0, 0)
-        alone(0, 1)
+        upper(0, 1)
         relus(0, 2)
-        relus(0, 3)
         sub(0, 0, 1)
+        both(0, 1)
         store(0, 0, 2)
-        alone(1, 0)
+        relus(0, 3)
+        upper(1, 0)
+        sub(0, 2, 3)
         relus(1, 1)
-        sub(0, 2, 4)
+        both(1, 0)
+        sub(0, 3, 4)
         store(0, 2, 4)
         relus(1, 2)
-        relus(1, 3)
-        cast("v", 0, 176, 256)
+        upper(1, 3)
         sub(1, 1, 2)
         store(1, 0, 2)
-        cast("s", 0, 0, 176)
-        sub(1, 2, 4)
+        cast("s", 0, 0, 256)
+        both(1, 3)
+        sub(1, 2, 3)
         store(1, 2, 4)
-        cast("v", 1, 0, 256)
         quant(0, 256)
+        cast("s", 1, 0, 128)
+        cast("v", 1, 128, 256)
         quant(256, 512)
         for q in range(4):
             eng = nc.scalar if q % 2 == 0 else nc.sync

@@ -18,8 +18,9 @@ ACT = mybir.ActivationFunctionType
 P = 128
 PACK = 4
 HALF = S // 2
-W_SPLIT = 48
-SR_SPLIT = 96
+W_SPLIT = 60
+SR_SPLIT = 48
+H_SPLIT = 96
 VECTOR_ALONE = {(1, 3)}
 
 
@@ -35,7 +36,7 @@ def tile_picked_ylista_soft_po_kernel(
         offs_t = keep.tile([P, S // 16], U16, name="offs_t")
         thr_t = keep.tile([P, PACK], F32, name="thr_t")
         neg_thr = keep.tile([P, PACK], F32, name="neg_thr")
-        mem_t = [keep.tile([P, U], F32, name=f"mem{j}") for j in range(PACK)]
+        mem_t = [keep.tile([P, U], F32, name=f"mem{j}", tag=f"mem{j}", align_bytes=64) for j in range(PACK)]
         sr_raw = keep.tile([P, PACK, N], F32, name="sr_raw")
         w1_raw = keep.tile([P, PACK, N], F32, name="w1_raw")
         xw_all = keep.tile([P, T], I32, name="xw_all")
@@ -44,51 +45,61 @@ def tile_picked_ylista_soft_po_kernel(
         nc.vector.memset(xs_all[:].bitcast(I32), 0)
         nc.sync.dma_start(slot_t[:], slot)
         mem_rows = mem.rearrange("(p j) u -> p j u", j=PACK)
-        for j in range(PACK):
+        for j in range(PACK - 1):
             nc.sync.dma_start(out=mem_t[j][:], in_=mem_rows[:, j, :])
         nc.sync.dma_start(offs_t[:], offs)
         for q in range(4):
-            nc.gpsimd.dma_start(
+            nc.sync.dma_start(
                 out=xs_all[32 * q : 32 * q + 4, :].bitcast(I32),
                 in_=x_scales[0, 4 * q : 4 * q + 4, :].bitcast(I32),
             )
         nc.sync.dma_start(out=sr_raw[:], in_=sr.rearrange("(p j) c -> p j c", j=PACK))
+        nc.sync.dma_start(out=mem_t[PACK - 1][:], in_=mem_rows[:, PACK - 1, :])
         nc.sync.dma_start(out=w1_raw[:], in_=w1.rearrange("(p j) c -> p j c", j=PACK))
-        nc.sync.dma_start(out=thr_t[:], in_=thr.rearrange("(p t) o -> p (t o)", t=PACK))
         nc.sync.dma_start(out=xw_all[:], in_=x_words[0].rearrange("p n t -> p (n t)").bitcast(I32))
-
-        h_rows = keep.tile([P, PACK, S], F32, name="h_rows")
-        for j in range(PACK - 1):
-            nc.vector.tensor_copy(h_rows[:, j, :], mem_t[j][:].indirect(slot_t[:]))
-        hs_bf = keep.tile([P, PACK * (S + N)], BF16, name="hs_bf", align_bytes=64)
-        for half in range(2):
-            cols = slice(half * HALF, (half + 1) * HALF)
-            nc.vector.tensor_copy(h_rows[:, PACK - 1, cols],
-                                  mem_t[PACK - 1][:].indirect(slot_t[:, half * (HALF // 16) : (half + 1) * (HALF // 16)]))
-            nc.scalar.copy(
-                out=hs_bf[:, PACK * half * HALF : PACK * (half + 1) * HALF].rearrange("p (c i t) -> p c t i", i=4, t=PACK),
-                in_=h_rows[:, :, cols].rearrange("p t (c i) -> p c t i", i=4),
-            )
-        xs_g = keep.tile([P, S], U8, name="xs_g", align_bytes=64)
-        nc.vector.tensor_copy(xs_g[:], xs_all[:].indirect(offs_t[:]))
+        nc.sync.dma_start(out=thr_t[:], in_=thr.rearrange("(p t) o -> p (t o)", t=PACK))
 
         def deal(dealt, raw, split):
             dst = dealt.rearrange("p (t m j) -> p m j t", t=PACK, j=PACK)
             src = raw[:].rearrange("p j (m t) -> p m j t", t=PACK)
-            if split < P:
-                nc.scalar.copy(out=dst[:, split:, :, :], in_=src[:, split:, :, :])
+            nc.scalar.copy(out=dst[:, split:, :, :], in_=src[:, split:, :, :])
             nc.vector.tensor_copy(out=dst[:, :split, :, :], in_=src[:, :split, :, :])
 
-        deal(hs_bf[:, PACK * S :], sr_raw, SR_SPLIT)
-        hs_codes = keep.tile([P, S + N], U32, name="hs_codes", align_bytes=64)
-        hs_scales = keep.tile([P, S + N], U8, name="hs_scales", align_bytes=64)
-        nc.vector.quantize_mx(out=hs_codes[:].bitcast(FP8X4), scales=hs_scales[:], in_=hs_bf[:])
-        h_codes, h_scales = hs_codes[:, :S], hs_scales[:, :S]
-        sr_codes, sr_scales = hs_codes[:, S:], hs_scales[:, S:]
+        h_rows = [keep.tile([P, PACK, HALF], F32, name=f"h_rows{half}") for half in range(2)]
+
+        def look_up(j):
+            for half in range(2):
+                nc.vector.tensor_copy(h_rows[half][:, j, :],
+                                      mem_t[j][:].indirect(slot_t[:, half * (HALF // 16) : (half + 1) * (HALF // 16)]))
+
+        for j in range(PACK - 1):
+            look_up(j)
+        xs_g = keep.tile([P, S], U8, name="xs_g", align_bytes=64)
+        nc.vector.tensor_copy(xs_g[:], xs_all[:].indirect(offs_t[:]))
+        sr_bf = keep.tile([P, PACK * N], BF16, name="sr_bf", align_bytes=64)
+        deal(sr_bf[:], sr_raw, SR_SPLIT)
+
+        h_bf = [keep.tile([P, HALF * PACK], BF16, name=f"h_bf{half}", align_bytes=64) for half in range(2)]
+
+        def weave(copy, dst, src, c0, c1):
+            copy(out=dst[:, PACK * c0 : PACK * c1].rearrange("p (c i t) -> p c t i", i=4, t=PACK),
+                 in_=src[:, :, c0:c1].rearrange("p t (c i) -> p c t i", i=4))
+
+        look_up(PACK - 1)
+        weave(nc.scalar.copy, h_bf[0], h_rows[0], 0, HALF)
+        sr_codes = keep.tile([P, N], U32, name="sr_codes", tag=f"mem{PACK - 1}", align_bytes=64)
+        sr_scales = keep.tile([P, N], U8, name="sr_scales", align_bytes=64)
+        nc.vector.quantize_mx(out=sr_codes[:].bitcast(FP8X4), scales=sr_scales[:], in_=sr_bf[:])
+        weave(nc.scalar.copy, h_bf[1], h_rows[1], 0, H_SPLIT)
+        weave(nc.vector.tensor_copy, h_bf[1], h_rows[1], H_SPLIT, HALF)
+        h_codes = keep.tile([P, S], U32, name="h_codes", align_bytes=64)
+        h_scales = keep.tile([P, S], U8, name="h_scales", align_bytes=64)
 
         acc = {}
         for half in range(2):
             cols = slice(half * HALF, (half + 1) * HALF)
+            nc.vector.quantize_mx(out=h_codes[:, cols].bitcast(FP8X4), scales=h_scales[:, cols],
+                                  in_=h_bf[half][:])
             for t in range(PACK):
                 rows = slice(t * P, (t + 1) * P)
                 acc[half, t] = psum.tile([P, HALF], F32, name=f"acc{half}{t}")
@@ -120,8 +131,8 @@ def tile_picked_ylista_soft_po_kernel(
         y = [keep.tile([P, PACK, HALF], F32, name=f"y{half}") for half in range(2)]
         up = [keep.tile([P, PACK, HALF], F32, name=f"up{half}") for half in range(2)]
         down = [keep.tile([P, PACK, HALF], F32, name=f"down{half}") for half in range(2)]
-        y_bf = keep.tile([P, S, PACK], BF16, name="y_bf", align_bytes=64)
-        y_codes = keep.tile([P, S], U32, name="y_codes", align_bytes=64)
+        y_bf = [keep.tile([P, HALF * PACK], BF16, name=f"y_bf{half}", align_bytes=64) for half in range(2)]
+        y_codes = [keep.tile([P, HALF], U32, name=f"y_codes{half}", align_bytes=64) for half in range(2)]
         y_scales = keep.tile([P, S], U8, name="y_scales", align_bytes=64)
 
         def relus(half, t):
@@ -145,17 +156,12 @@ def tile_picked_ylista_soft_po_kernel(
             nc.sync.dma_start(out=out_rows[:, t0:t1, half * HALF : (half + 1) * HALF], in_=y[half][:, t0:t1, :])
 
         def cast(eng, half, c0, c1):
-            dst = y_bf[:, half * HALF + c0 : half * HALF + c1, :].rearrange("p (c i) t -> p c t i", i=4)
-            src = y[half][:, :, c0:c1].rearrange("p t (c i) -> p c t i", i=4)
-            if eng == "v":
-                nc.vector.tensor_copy(out=dst, in_=src)
-            else:
-                nc.scalar.copy(out=dst, in_=src)
+            weave(nc.vector.tensor_copy if eng == "v" else nc.scalar.copy, y_bf[half], y[half], c0, c1)
 
         def quant(c0, c1):
-            nc.vector.quantize_mx(out=y_codes[:, c0:c1].bitcast(FP8X4), scales=y_scales[:, c0:c1],
-                                  in_=y_bf[:, c0:c1, :].rearrange("p c t -> p (c t)"))
-            nc.sync.dma_start(out=out_words[:, c0:c1], in_=y_codes[:, c0:c1].bitcast(I32))
+            half = c0 // HALF
+            nc.vector.quantize_mx(out=y_codes[half][:].bitcast(FP8X4), scales=y_scales[:, c0:c1], in_=y_bf[half][:])
+            nc.sync.dma_start(out=out_words[:, c0:c1], in_=y_codes[half][:].bitcast(I32))
 
         relus(0, 0)
         upper(0, 1)

@@ -20,7 +20,7 @@ PACK = 4
 HALF = S // 2
 W_SPLIT = 60
 SR_SPLIT = 48
-H_SPLIT = 96
+H_SPLIT = 144
 VECTOR_ALONE = {(1, 3)}
 
 
@@ -42,75 +42,77 @@ def tile_picked_ylista_soft_po_kernel(
         xw_all = keep.tile([P, T], I32, name="xw_all")
         xs_all = keep.tile([P, T], U8, name="xs_all")
 
+        xs_g = keep.tile([P, S], U8, name="xs_g", align_bytes=64)
         nc.vector.memset(xs_all[:].bitcast(I32), 0)
-        nc.sync.dma_start(slot_t[:], slot)
+        nc.vector.memset(xs_g[:].bitcast(I32), 0)
         mem_rows = mem.rearrange("(p j) u -> p j u", j=PACK)
-        for j in range(PACK - 1):
+        nc.sync.dma_start(out=mem_t[0][:], in_=mem_rows[:, 0, :])
+        nc.sync.dma_start(slot_t[:], slot)
+        for j in range(1, PACK - 1):
             nc.sync.dma_start(out=mem_t[j][:], in_=mem_rows[:, j, :])
         nc.sync.dma_start(offs_t[:], offs)
-        for q in range(4):
-            nc.sync.dma_start(
-                out=xs_all[32 * q : 32 * q + 4, :].bitcast(I32),
-                in_=x_scales[0, 4 * q : 4 * q + 4, :].bitcast(I32),
-            )
+        nc.sync.dma_start(out=xs_all[0:P:8, :].bitcast(I32), in_=x_scales[0].bitcast(I32))
         nc.sync.dma_start(out=sr_raw[:], in_=sr.rearrange("(p j) c -> p j c", j=PACK))
         nc.sync.dma_start(out=mem_t[PACK - 1][:], in_=mem_rows[:, PACK - 1, :])
         nc.sync.dma_start(out=w1_raw[:], in_=w1.rearrange("(p j) c -> p j c", j=PACK))
         nc.sync.dma_start(out=xw_all[:], in_=x_words[0].rearrange("p n t -> p (n t)").bitcast(I32))
         nc.sync.dma_start(out=thr_t[:], in_=thr.rearrange("(p t) o -> p (t o)", t=PACK))
 
-        def deal(dealt, raw, split):
-            dst = dealt.rearrange("p (t m j) -> p m j t", t=PACK, j=PACK)
-            src = raw[:].rearrange("p j (m t) -> p m j t", t=PACK)
-            nc.scalar.copy(out=dst[:, split:, :, :], in_=src[:, split:, :, :])
-            nc.vector.tensor_copy(out=dst[:, :split, :, :], in_=src[:, :split, :, :])
+        def deal(copy, dealt, raw, t0):
+            copy(out=dealt.rearrange("p (t m j) -> p m j t", t=2, j=PACK),
+                 in_=raw[:].rearrange("p j (m t) -> p m j t", t=PACK)[:, :, :, t0 : t0 + 2])
 
-        h_rows = [keep.tile([P, PACK, HALF], F32, name=f"h_rows{half}") for half in range(2)]
-
-        def look_up(j):
-            for half in range(2):
-                nc.vector.tensor_copy(h_rows[half][:, j, :],
-                                      mem_t[j][:].indirect(slot_t[:, half * (HALF // 16) : (half + 1) * (HALF // 16)]))
-
+        h_rows = keep.tile([P, PACK, S], F32, name="h_rows")
         for j in range(PACK - 1):
-            look_up(j)
-        xs_g = keep.tile([P, S], U8, name="xs_g", align_bytes=64)
-        nc.vector.tensor_copy(xs_g[:], xs_all[:].indirect(offs_t[:]))
+            nc.vector.tensor_copy(h_rows[:, j, :], mem_t[j][:].indirect(slot_t[:]))
+        xs_picked = keep.tile([P, S], U8, name="xs_picked", align_bytes=64)
+        nc.vector.tensor_copy(xs_picked[:], xs_all[:].indirect(offs_t[:]))
         sr_bf = keep.tile([P, PACK * N], BF16, name="sr_bf", align_bytes=64)
-        deal(sr_bf[:], sr_raw, SR_SPLIT)
+        deal(nc.vector.tensor_copy, sr_bf[:, : 2 * N], sr_raw, 0)
+        deal(nc.scalar.copy, sr_bf[:, 2 * N :], sr_raw, 2)
+        for r in range(4):
+            nc.sync.dma_start(out=xs_g[r:P:32, :].bitcast(I32), in_=xs_picked[8 * r : P : 32, :].bitcast(I32))
 
-        h_bf = [keep.tile([P, HALF * PACK], BF16, name=f"h_bf{half}", align_bytes=64) for half in range(2)]
+        h_bf0 = keep.tile([P, HALF * PACK], BF16, name="h_bf0", tag="h_bf0", align_bytes=64)
 
         def weave(copy, dst, src, c0, c1):
             copy(out=dst[:, PACK * c0 : PACK * c1].rearrange("p (c i t) -> p c t i", i=4, t=PACK),
                  in_=src[:, :, c0:c1].rearrange("p t (c i) -> p c t i", i=4))
 
-        look_up(PACK - 1)
-        weave(nc.scalar.copy, h_bf[0], h_rows[0], 0, HALF)
+        for half in range(2):
+            nc.vector.tensor_copy(h_rows[:, PACK - 1, half * HALF : (half + 1) * HALF],
+                                  mem_t[PACK - 1][:].indirect(slot_t[:, half * (HALF // 16) : (half + 1) * (HALF // 16)]))
+        weave(nc.scalar.copy, h_bf0, h_rows[:, :, :HALF], 0, HALF)
         sr_codes = keep.tile([P, N], U32, name="sr_codes", tag=f"mem{PACK - 1}", align_bytes=64)
         sr_scales = keep.tile([P, N], U8, name="sr_scales", align_bytes=64)
         nc.vector.quantize_mx(out=sr_codes[:].bitcast(FP8X4), scales=sr_scales[:], in_=sr_bf[:])
-        weave(nc.scalar.copy, h_bf[1], h_rows[1], 0, H_SPLIT)
-        weave(nc.vector.tensor_copy, h_bf[1], h_rows[1], H_SPLIT, HALF)
         h_codes = keep.tile([P, S], U32, name="h_codes", align_bytes=64)
         h_scales = keep.tile([P, S], U8, name="h_scales", align_bytes=64)
-
         acc = {}
-        for half in range(2):
+
+        def first_pass(half, h_bf):
             cols = slice(half * HALF, (half + 1) * HALF)
-            nc.vector.quantize_mx(out=h_codes[:, cols].bitcast(FP8X4), scales=h_scales[:, cols],
-                                  in_=h_bf[half][:])
+            nc.vector.quantize_mx(out=h_codes[:, cols].bitcast(FP8X4), scales=h_scales[:, cols], in_=h_bf[:])
             for t in range(PACK):
                 rows = slice(t * P, (t + 1) * P)
                 acc[half, t] = psum.tile([P, HALF], F32, name=f"acc{half}{t}")
                 nc.tensor.matmul_mx(out=acc[half, t][:], lhsT=sr_codes[:, rows].bitcast(FP8X4),
                                     lhsT_scale=sr_scales[:, rows], rhs=h_codes[:, cols].bitcast(FP8X4),
                                     rhs_scale=h_scales[:, cols], start=True, stop=False)
-        w1_bf = keep.tile([P, PACK * N], BF16, name="w1_bf", align_bytes=64)
-        deal(w1_bf[:], w1_raw, W_SPLIT)
+
+        first_pass(0, h_bf0)
+        h_bf1 = keep.tile([P, HALF * PACK], BF16, name="h_bf1", align_bytes=64)
+        weave(nc.scalar.copy, h_bf1, h_rows[:, :, HALF:], 0, HALF)
+        first_pass(1, h_bf1)
+        w1_bf0 = keep.tile([P, 2 * N], BF16, name="w1_bf0", tag="h_bf0", align_bytes=64)
+        w1_bf1 = keep.tile([P, 2 * N], BF16, name="w1_bf1", align_bytes=64)
+        deal(nc.vector.tensor_copy, w1_bf0[:], w1_raw, 0)
+        deal(nc.scalar.copy, w1_bf1[:], w1_raw, 2)
         w1_codes = keep.tile([P, N], U32, name="w1_codes", align_bytes=64)
         w1_scales = keep.tile([P, N], U8, name="w1_scales", align_bytes=64)
-        nc.vector.quantize_mx(out=w1_codes[:].bitcast(FP8X4), scales=w1_scales[:], in_=w1_bf[:])
+        for pair, w1_bf in enumerate((w1_bf0, w1_bf1)):
+            rows = slice(pair * 2 * P, (pair + 1) * 2 * P)
+            nc.vector.quantize_mx(out=w1_codes[:, rows].bitcast(FP8X4), scales=w1_scales[:, rows], in_=w1_bf[:])
 
         nc.scalar.activation(out=neg_thr[:], in_=thr_t[:], func=ACT.Copy, scale=-1.0)
         xw_g = []

@@ -18,10 +18,10 @@ ACT = mybir.ActivationFunctionType
 P = 128
 PACK = 4
 HALF = S // 2
-W_SPLIT = 60
-SR_SPLIT = 48
-H_SPLIT = 144
-VECTOR_ALONE = {(1, 3)}
+LIST_HALF = HALF // 16
+RUN = 4
+SCALE_STEP = P // 16
+LAST_ON_SCALAR = 80
 
 
 def tile_picked_ylista_soft_po_kernel(
@@ -32,6 +32,24 @@ def tile_picked_ylista_soft_po_kernel(
         keep = ctx.enter_context(tc.tile_pool(name="keep", bufs=1))
         psum = ctx.enter_context(tc.psum_pool(name="psum", bufs=1))
 
+        def half_cols(half):
+            return slice(half * HALF, (half + 1) * HALF)
+
+        def list_half(tile, half):
+            return tile[:, half * LIST_HALF : (half + 1) * LIST_HALF]
+
+        def weave(copy, dst, src, c0, c1):
+            copy(
+                out=dst[:, PACK * c0 : PACK * c1].rearrange("p (c i t) -> p c t i", i=RUN, t=PACK),
+                in_=src[:, :, c0:c1].rearrange("p t (c i) -> p c t i", i=RUN),
+            )
+
+        def deal(copy, dst, raw, t0):
+            copy(
+                out=dst.rearrange("p (t m j) -> p m j t", t=2, j=PACK),
+                in_=raw[:].rearrange("p j (m t) -> p m j t", t=PACK)[:, :, :, t0 : t0 + 2],
+            )
+
         slot_t = keep.tile([P, S // 16], U16, name="slot_t")
         offs_t = keep.tile([P, S // 16], U16, name="offs_t")
         thr_t = keep.tile([P, PACK], F32, name="thr_t")
@@ -39,71 +57,73 @@ def tile_picked_ylista_soft_po_kernel(
         mem_t = [keep.tile([P, U], F32, name=f"mem{j}", tag=f"mem{j}", align_bytes=64) for j in range(PACK)]
         sr_raw = keep.tile([P, PACK, N], F32, name="sr_raw")
         w1_raw = keep.tile([P, PACK, N], F32, name="w1_raw")
-        xw_all = keep.tile([P, T], I32, name="xw_all")
-        xs_all = keep.tile([P, T], U8, name="xs_all")
+        xs_all = keep.tile([P, T], U8, name="xs_all", tag="x")
+        x_scale = keep.tile([P, S], U8, name="x_scale", align_bytes=64)
 
-        xs_g = keep.tile([P, S], U8, name="xs_g", align_bytes=64)
         nc.vector.memset(xs_all[:].bitcast(I32), 0)
-        nc.vector.memset(xs_g[:].bitcast(I32), 0)
+        nc.vector.memset(x_scale[:].bitcast(I32), 0)
         mem_rows = mem.rearrange("(p j) u -> p j u", j=PACK)
         nc.sync.dma_start(out=mem_t[0][:], in_=mem_rows[:, 0, :])
         nc.sync.dma_start(slot_t[:], slot)
-        for j in range(1, PACK - 1):
-            nc.sync.dma_start(out=mem_t[j][:], in_=mem_rows[:, j, :])
+        nc.sync.dma_start(out=mem_t[1][:], in_=mem_rows[:, 1, :])
         nc.sync.dma_start(offs_t[:], offs)
-        nc.sync.dma_start(out=xs_all[0:P:8, :].bitcast(I32), in_=x_scales[0].bitcast(I32))
-        nc.sync.dma_start(out=sr_raw[:], in_=sr.rearrange("(p j) c -> p j c", j=PACK))
-        nc.sync.dma_start(out=mem_t[PACK - 1][:], in_=mem_rows[:, PACK - 1, :])
-        nc.sync.dma_start(out=w1_raw[:], in_=w1.rearrange("(p j) c -> p j c", j=PACK))
-        nc.sync.dma_start(out=xw_all[:], in_=x_words[0].rearrange("p n t -> p (n t)").bitcast(I32))
+        nc.sync.dma_start(out=xs_all[0:P:SCALE_STEP, :].bitcast(I32), in_=x_scales[0].bitcast(I32))
         nc.sync.dma_start(out=thr_t[:], in_=thr.rearrange("(p t) o -> p (t o)", t=PACK))
-
-        def deal(copy, dealt, raw, t0):
-            copy(out=dealt.rearrange("p (t m j) -> p m j t", t=2, j=PACK),
-                 in_=raw[:].rearrange("p j (m t) -> p m j t", t=PACK)[:, :, :, t0 : t0 + 2])
+        nc.sync.dma_start(out=mem_t[2][:], in_=mem_rows[:, 2, :])
+        nc.sync.dma_start(out=sr_raw[:], in_=sr.rearrange("(p j) c -> p j c", j=PACK))
+        nc.sync.dma_start(out=mem_t[3][:], in_=mem_rows[:, 3, :])
+        nc.sync.dma_start(out=w1_raw[:], in_=w1.rearrange("(p j) c -> p j c", j=PACK))
+        nc.scalar.activation(out=neg_thr[:], in_=thr_t[:], func=ACT.Copy, scale=-1.0)
 
         h_rows = keep.tile([P, PACK, S], F32, name="h_rows")
-        for j in range(PACK - 1):
+        for j in range(2):
             nc.vector.tensor_copy(h_rows[:, j, :], mem_t[j][:].indirect(slot_t[:]))
         xs_picked = keep.tile([P, S], U8, name="xs_picked", align_bytes=64)
         nc.vector.tensor_copy(xs_picked[:], xs_all[:].indirect(offs_t[:]))
+        for r in range(4):
+            nc.sync.dma_start(
+                out=x_scale[r:P:32, :].bitcast(I32), in_=xs_picked[SCALE_STEP * r : P : 32, :].bitcast(I32)
+            )
+        xw_all = keep.tile([P, T], I32, name="xw_all", tag="x")
+        nc.sync.dma_start(out=xw_all[:], in_=x_words[0].rearrange("p n t -> p (n t)").bitcast(I32))
+        nc.vector.tensor_copy(h_rows[:, 2, :], mem_t[2][:].indirect(slot_t[:]))
         sr_bf = keep.tile([P, PACK * N], BF16, name="sr_bf", align_bytes=64)
         deal(nc.vector.tensor_copy, sr_bf[:, : 2 * N], sr_raw, 0)
         deal(nc.scalar.copy, sr_bf[:, 2 * N :], sr_raw, 2)
-        for r in range(4):
-            nc.sync.dma_start(out=xs_g[r:P:32, :].bitcast(I32), in_=xs_picked[8 * r : P : 32, :].bitcast(I32))
 
         h_bf0 = keep.tile([P, HALF * PACK], BF16, name="h_bf0", tag="h_bf0", align_bytes=64)
-
-        def weave(copy, dst, src, c0, c1):
-            copy(out=dst[:, PACK * c0 : PACK * c1].rearrange("p (c i t) -> p c t i", i=4, t=PACK),
-                 in_=src[:, :, c0:c1].rearrange("p t (c i) -> p c t i", i=4))
-
         for half in range(2):
-            nc.vector.tensor_copy(h_rows[:, PACK - 1, half * HALF : (half + 1) * HALF],
-                                  mem_t[PACK - 1][:].indirect(slot_t[:, half * (HALF // 16) : (half + 1) * (HALF // 16)]))
-        weave(nc.scalar.copy, h_bf0, h_rows[:, :, :HALF], 0, HALF)
-        sr_codes = keep.tile([P, N], U32, name="sr_codes", tag=f"mem{PACK - 1}", align_bytes=64)
+            nc.vector.tensor_copy(h_rows[:, 3, half_cols(half)], mem_t[3][:].indirect(list_half(slot_t, half)))
+        weave(nc.scalar.copy, h_bf0, h_rows[:, :, half_cols(0)], 0, HALF)
+        sr_codes = keep.tile([P, N], U32, name="sr_codes", tag="mem3", align_bytes=64)
         sr_scales = keep.tile([P, N], U8, name="sr_scales", align_bytes=64)
         nc.vector.quantize_mx(out=sr_codes[:].bitcast(FP8X4), scales=sr_scales[:], in_=sr_bf[:])
+
         h_codes = keep.tile([P, S], U32, name="h_codes", align_bytes=64)
         h_scales = keep.tile([P, S], U8, name="h_scales", align_bytes=64)
         acc = {}
 
-        def first_pass(half, h_bf):
-            cols = slice(half * HALF, (half + 1) * HALF)
+        def open_groups(half, h_bf):
+            cols = half_cols(half)
             nc.vector.quantize_mx(out=h_codes[:, cols].bitcast(FP8X4), scales=h_scales[:, cols], in_=h_bf[:])
             for t in range(PACK):
                 rows = slice(t * P, (t + 1) * P)
                 acc[half, t] = psum.tile([P, HALF], F32, name=f"acc{half}{t}")
-                nc.tensor.matmul_mx(out=acc[half, t][:], lhsT=sr_codes[:, rows].bitcast(FP8X4),
-                                    lhsT_scale=sr_scales[:, rows], rhs=h_codes[:, cols].bitcast(FP8X4),
-                                    rhs_scale=h_scales[:, cols], start=True, stop=False)
+                nc.tensor.matmul_mx(
+                    out=acc[half, t][:],
+                    lhsT=sr_codes[:, rows].bitcast(FP8X4),
+                    lhsT_scale=sr_scales[:, rows],
+                    rhs=h_codes[:, cols].bitcast(FP8X4),
+                    rhs_scale=h_scales[:, cols],
+                    start=True,
+                    stop=False,
+                )
 
-        first_pass(0, h_bf0)
+        open_groups(0, h_bf0)
         h_bf1 = keep.tile([P, HALF * PACK], BF16, name="h_bf1", align_bytes=64)
-        weave(nc.scalar.copy, h_bf1, h_rows[:, :, HALF:], 0, HALF)
-        first_pass(1, h_bf1)
+        weave(nc.scalar.copy, h_bf1, h_rows[:, :, half_cols(1)], 0, HALF)
+        open_groups(1, h_bf1)
+
         w1_bf0 = keep.tile([P, 2 * N], BF16, name="w1_bf0", tag="h_bf0", align_bytes=64)
         w1_bf1 = keep.tile([P, 2 * N], BF16, name="w1_bf1", align_bytes=64)
         deal(nc.vector.tensor_copy, w1_bf0[:], w1_raw, 0)
@@ -114,83 +134,81 @@ def tile_picked_ylista_soft_po_kernel(
             rows = slice(pair * 2 * P, (pair + 1) * 2 * P)
             nc.vector.quantize_mx(out=w1_codes[:, rows].bitcast(FP8X4), scales=w1_scales[:, rows], in_=w1_bf[:])
 
-        nc.scalar.activation(out=neg_thr[:], in_=thr_t[:], func=ACT.Copy, scale=-1.0)
-        xw_g = []
+        x_codes = [keep.tile([P, HALF], U32, name=f"x_codes{half}", align_bytes=64) for half in range(2)]
         for half in range(2):
-            g = keep.tile([P, HALF], U32, name=f"xw_g{half}", align_bytes=64)
-            nc.vector.tensor_copy(g[:], xw_all[:].bitcast(U32).indirect(offs_t[:, half * (HALF // 16) : (half + 1) * (HALF // 16)]))
-            xw_g.append(g)
+            nc.vector.tensor_copy(x_codes[half][:], xw_all[:].bitcast(U32).indirect(list_half(offs_t, half)))
         for half in range(2):
-            cols = slice(half * HALF, (half + 1) * HALF)
-            for t in range(PACK):
+            for t in (0, 1, 3, 2):
                 rows = slice(t * P, (t + 1) * P)
-                nc.tensor.matmul_mx(out=acc[half, t][:], lhsT=w1_codes[:, rows].bitcast(FP8X4),
-                                    lhsT_scale=w1_scales[:, rows], rhs=xw_g[half][:].bitcast(FP8X4),
-                                    rhs_scale=xs_g[:, cols], start=False, stop=True)
+                nc.tensor.matmul_mx(
+                    out=acc[half, t][:],
+                    lhsT=w1_codes[:, rows].bitcast(FP8X4),
+                    lhsT_scale=w1_scales[:, rows],
+                    rhs=x_codes[half][:].bitcast(FP8X4),
+                    rhs_scale=x_scale[:, half_cols(half)],
+                    start=False,
+                    stop=True,
+                )
 
         out_rows = out_0.rearrange("(p t) j -> p t j", t=PACK)
         out_words = out_1[0].rearrange("p n t -> p (n t)").bitcast(I32)
-        y = [keep.tile([P, PACK, HALF], F32, name=f"y{half}") for half in range(2)]
+        res = [keep.tile([P, PACK, HALF], F32, name=f"res{half}") for half in range(2)]
         up = [keep.tile([P, PACK, HALF], F32, name=f"up{half}") for half in range(2)]
-        down = [keep.tile([P, PACK, HALF], F32, name=f"down{half}") for half in range(2)]
-        y_bf = [keep.tile([P, HALF * PACK], BF16, name=f"y_bf{half}", align_bytes=64) for half in range(2)]
-        y_codes = [keep.tile([P, HALF], U32, name=f"y_codes{half}", align_bytes=64) for half in range(2)]
-        y_scales = keep.tile([P, S], U8, name="y_scales", align_bytes=64)
+        down = [keep.tile([P, 2, HALF], F32, name=f"down{half}") for half in range(2)]
+        res_bf = [keep.tile([P, HALF * PACK], BF16, name=f"res_bf{half}", align_bytes=64) for half in range(2)]
+        res_codes = [keep.tile([P, HALF], U32, name=f"res_codes{half}", align_bytes=64) for half in range(2)]
+        res_scales = keep.tile([P, S], U8, name="res_scales", align_bytes=64)
 
         def relus(half, t):
-            a = acc[half, t]
-            nc.scalar.activation(out=up[half][:, t, :], in_=a[:], func=ACT.Relu, bias=thr_t[:, t : t + 1], scale=1.0)
-            nc.scalar.activation(out=down[half][:, t, :], in_=a[:], func=ACT.Relu, bias=thr_t[:, t : t + 1], scale=-1.0)
+            bias = thr_t[:, t : t + 1]
+            nc.scalar.activation(out=up[half][:, t, :], in_=acc[half, t][:], func=ACT.Relu, bias=bias, scale=1.0)
+            nc.scalar.activation(out=down[half][:, t // 2, :], in_=acc[half, t][:], func=ACT.Relu, bias=bias, scale=-1.0)
 
-        def sub(half, t0, t1):
-            nc.vector.tensor_tensor(y[half][:, t0:t1, :], up[half][:, t0:t1, :], down[half][:, t0:t1, :], ALU.subtract)
+        def subtract(engine, half, t):
+            engine.tensor_tensor(res[half][:, t, :], up[half][:, t, :], down[half][:, t // 2, :], ALU.subtract)
 
-        def upper(half, t):
-            a = acc[half, t]
-            nc.vector.tensor_scalar(out=up[half][:, t, :], in0=a[:], scalar1=neg_thr[:, t : t + 1], scalar2=None, op0=ALU.max)
+        def clip_below(half, t):
+            nc.vector.tensor_scalar(
+                out=up[half][:, t, :], in0=acc[half, t][:], scalar1=neg_thr[:, t : t + 1], scalar2=None, op0=ALU.max
+            )
 
-        def both(half, t):
-            a = acc[half, t]
-            nc.vector.scalar_tensor_tensor(out=y[half][:, t, :], in0=a[:], scalar=thr_t[:, t : t + 1], in1=up[half][:, t, :],
-                                           op0=ALU.min, op1=ALU.add)
+        def clip_above_and_add(half, t):
+            nc.vector.scalar_tensor_tensor(
+                out=res[half][:, t, :],
+                in0=acc[half, t][:],
+                scalar=thr_t[:, t : t + 1],
+                in1=up[half][:, t, :],
+                op0=ALU.min,
+                op1=ALU.add,
+            )
 
-        def store(half, t0, t1):
-            nc.sync.dma_start(out=out_rows[:, t0:t1, half * HALF : (half + 1) * HALF], in_=y[half][:, t0:t1, :])
+        def store_pair(half, t0):
+            nc.sync.dma_start(out=out_rows[:, t0 : t0 + 2, half_cols(half)], in_=res[half][:, t0 : t0 + 2, :])
 
-        def cast(eng, half, c0, c1):
-            weave(nc.vector.tensor_copy if eng == "v" else nc.scalar.copy, y_bf[half], y[half], c0, c1)
+        for half in range(2):
+            relus(half, 0)
+            clip_below(half, 1)
+            clip_below(half, 3)
+            relus(half, 2)
+            clip_above_and_add(half, 1)
+            subtract(nc.gpsimd, half, 0)
+            store_pair(half, 0)
+            clip_above_and_add(half, 3)
+            if half == 0:
+                subtract(nc.gpsimd, half, 2)
+            else:
+                weave(nc.scalar.copy, res_bf[0], res[0], 0, HALF)
+                subtract(nc.vector, half, 2)
+            store_pair(half, 2)
+        weave(nc.vector.tensor_copy, res_bf[1], res[1], LAST_ON_SCALAR, HALF)
+        weave(nc.scalar.copy, res_bf[1], res[1], 0, LAST_ON_SCALAR)
 
-        def quant(c0, c1):
-            half = c0 // HALF
-            nc.vector.quantize_mx(out=y_codes[half][:].bitcast(FP8X4), scales=y_scales[:, c0:c1], in_=y_bf[half][:])
-            nc.sync.dma_start(out=out_words[:, c0:c1], in_=y_codes[half][:].bitcast(I32))
-
-        relus(0, 0)
-        upper(0, 1)
-        relus(0, 2)
-        sub(0, 0, 1)
-        both(0, 1)
-        store(0, 0, 2)
-        relus(0, 3)
-        upper(1, 0)
-        sub(0, 2, 3)
-        relus(1, 1)
-        both(1, 0)
-        sub(0, 3, 4)
-        store(0, 2, 4)
-        relus(1, 2)
-        upper(1, 3)
-        sub(1, 1, 2)
-        store(1, 0, 2)
-        cast("s", 0, 0, 256)
-        both(1, 3)
-        sub(1, 2, 3)
-        store(1, 2, 4)
-        quant(0, 256)
-        cast("s", 1, 0, 128)
-        cast("v", 1, 128, 256)
-        quant(256, 512)
+        for half in range(2):
+            cols = half_cols(half)
+            nc.vector.quantize_mx(out=res_codes[half][:].bitcast(FP8X4), scales=res_scales[:, cols], in_=res_bf[half][:])
+            nc.sync.dma_start(out=out_words[:, cols], in_=res_codes[half][:].bitcast(I32))
         for q in range(4):
-            eng = nc.scalar if q % 2 == 0 else nc.sync
-            eng.dma_start(out=out_2[0, 4 * q : 4 * q + 4, :].bitcast(I32),
-                          in_=y_scales[32 * q : 32 * q + 4, :].bitcast(I32))
+            queue = nc.scalar if q % 2 == 0 else nc.sync
+            queue.dma_start(
+                out=out_2[0, 4 * q : 4 * q + 4, :].bitcast(I32), in_=res_scales[32 * q : 32 * q + 4, :].bitcast(I32)
+            )

@@ -38,6 +38,9 @@ def tile_picked_ylista_soft_po_kernel(
         def list_half(tile, half):
             return tile[:, half * LIST_HALF : (half + 1) * LIST_HALF]
 
+        def scalar_round(out, in_):
+            nc.scalar.activation(out=out, in_=in_, func=ACT.Copy)
+
         def weave(copy, dst, src, c0, c1):
             copy(
                 out=dst[:, PACK * c0 : PACK * c1].rearrange("p (c i t) -> p c t i", i=RUN, t=PACK),
@@ -57,7 +60,8 @@ def tile_picked_ylista_soft_po_kernel(
         mem_t = [keep.tile([P, U], F32, name=f"mem{j}", tag=f"mem{j}", align_bytes=64) for j in range(PACK)]
         sr_raw = keep.tile([P, PACK, N], F32, name="sr_raw")
         w1_raw = keep.tile([P, PACK, N], F32, name="w1_raw")
-        xs_all = keep.tile([P, T], U8, name="xs_all", tag="x")
+        xs_all = keep.tile([P, T], U8, name="xs_all")
+        xw_all = keep.tile([P, T], I32, name="xw_all")
         x_scale = keep.tile([P, S], U8, name="x_scale", align_bytes=64)
 
         nc.vector.memset(xs_all[:].bitcast(I32), 0)
@@ -65,66 +69,66 @@ def tile_picked_ylista_soft_po_kernel(
         mem_rows = mem.rearrange("(p j) u -> p j u", j=PACK)
         nc.sync.dma_start(out=mem_t[0][:], in_=mem_rows[:, 0, :])
         nc.sync.dma_start(slot_t[:], slot)
-        nc.sync.dma_start(out=mem_t[1][:], in_=mem_rows[:, 1, :])
+        for j in range(1, PACK):
+            nc.sync.dma_start(out=mem_t[j][:], in_=mem_rows[:, j, :])
         nc.sync.dma_start(offs_t[:], offs)
         nc.sync.dma_start(out=xs_all[0:P:SCALE_STEP, :].bitcast(I32), in_=x_scales[0].bitcast(I32))
-        nc.sync.dma_start(out=thr_t[:], in_=thr.rearrange("(p t) o -> p (t o)", t=PACK))
-        nc.sync.dma_start(out=mem_t[2][:], in_=mem_rows[:, 2, :])
         nc.sync.dma_start(out=sr_raw[:], in_=sr.rearrange("(p j) c -> p j c", j=PACK))
-        nc.sync.dma_start(out=mem_t[3][:], in_=mem_rows[:, 3, :])
         nc.sync.dma_start(out=w1_raw[:], in_=w1.rearrange("(p j) c -> p j c", j=PACK))
-        nc.scalar.activation(out=neg_thr[:], in_=thr_t[:], func=ACT.Copy, scale=-1.0)
+        nc.sync.dma_start(out=xw_all[:], in_=x_words[0].rearrange("p n t -> p (n t)").bitcast(I32))
+        nc.sync.dma_start(out=thr_t[:], in_=thr.rearrange("(p t) o -> p (t o)", t=PACK))
 
         h_rows = keep.tile([P, PACK, S], F32, name="h_rows")
-        for j in range(2):
+        for j in range(3):
             nc.vector.tensor_copy(h_rows[:, j, :], mem_t[j][:].indirect(slot_t[:]))
+        h_bf0 = keep.tile([P, HALF * PACK], BF16, name="h_bf0", align_bytes=64)
+        h_bf1 = keep.tile([P, HALF * PACK], BF16, name="h_bf1", align_bytes=64)
+        for half in range(2):
+            nc.vector.tensor_copy(h_rows[:, 3, half_cols(half)], mem_t[3][:].indirect(list_half(slot_t, half)))
+        weave(scalar_round, h_bf0, h_rows[:, :, half_cols(0)], 0, HALF)
+        nc.gpsimd.tensor_scalar(
+            out=h_bf1[:].rearrange("p (c t) -> p c t", t=PACK),
+            in0=h_rows[:, :, half_cols(1)].rearrange("p t c -> p c t"),
+            scalar1=1.0,
+            scalar2=0.0,
+            op0=ALU.mult,
+            op1=ALU.add,
+        )
         xs_picked = keep.tile([P, S], U8, name="xs_picked", align_bytes=64)
         nc.vector.tensor_copy(xs_picked[:], xs_all[:].indirect(offs_t[:]))
         for r in range(4):
             nc.sync.dma_start(
                 out=x_scale[r:P:32, :].bitcast(I32), in_=xs_picked[SCALE_STEP * r : P : 32, :].bitcast(I32)
             )
-        xw_all = keep.tile([P, T], I32, name="xw_all", tag="x")
-        nc.sync.dma_start(out=xw_all[:], in_=x_words[0].rearrange("p n t -> p (n t)").bitcast(I32))
-        nc.vector.tensor_copy(h_rows[:, 2, :], mem_t[2][:].indirect(slot_t[:]))
-        sr_bf = keep.tile([P, PACK * N], BF16, name="sr_bf", align_bytes=64)
-        deal(nc.vector.tensor_copy, sr_bf[:, : 2 * N], sr_raw, 0)
-        deal(nc.scalar.copy, sr_bf[:, 2 * N :], sr_raw, 2)
-
-        h_bf0 = keep.tile([P, HALF * PACK], BF16, name="h_bf0", tag="h_bf0", align_bytes=64)
-        for half in range(2):
-            nc.vector.tensor_copy(h_rows[:, 3, half_cols(half)], mem_t[3][:].indirect(list_half(slot_t, half)))
-        weave(nc.scalar.copy, h_bf0, h_rows[:, :, half_cols(0)], 0, HALF)
-        sr_codes = keep.tile([P, N], U32, name="sr_codes", tag="mem3", align_bytes=64)
-        sr_scales = keep.tile([P, N], U8, name="sr_scales", align_bytes=64)
-        nc.vector.quantize_mx(out=sr_codes[:].bitcast(FP8X4), scales=sr_scales[:], in_=sr_bf[:])
-
         h_codes = keep.tile([P, S], U32, name="h_codes", align_bytes=64)
         h_scales = keep.tile([P, S], U8, name="h_scales", align_bytes=64)
-        acc = {}
-
-        def open_groups(half, h_bf):
+        for half, h_bf in enumerate((h_bf0, h_bf1)):
             cols = half_cols(half)
             nc.vector.quantize_mx(out=h_codes[:, cols].bitcast(FP8X4), scales=h_scales[:, cols], in_=h_bf[:])
-            for t in range(PACK):
-                rows = slice(t * P, (t + 1) * P)
-                acc[half, t] = psum.tile([P, HALF], F32, name=f"acc{half}{t}")
-                nc.tensor.matmul_mx(
-                    out=acc[half, t][:],
-                    lhsT=sr_codes[:, rows].bitcast(FP8X4),
-                    lhsT_scale=sr_scales[:, rows],
-                    rhs=h_codes[:, cols].bitcast(FP8X4),
-                    rhs_scale=h_scales[:, cols],
-                    start=True,
-                    stop=False,
-                )
+        sr_codes = keep.tile([P, N], U32, name="sr_codes", align_bytes=64)
+        sr_scales = keep.tile([P, N], U8, name="sr_scales", align_bytes=64)
+        acc = {}
+        for pair in range(2):
+            sr_bf = keep.tile([P, 2 * N], BF16, name=f"sr_bf{pair}", align_bytes=64)
+            deal(nc.scalar.copy, sr_bf[:], sr_raw, 2 * pair)
+            rows = slice(pair * 2 * P, (pair + 1) * 2 * P)
+            nc.vector.quantize_mx(out=sr_codes[:, rows].bitcast(FP8X4), scales=sr_scales[:, rows], in_=sr_bf[:])
+            for half in range(2):
+                cols = half_cols(half)
+                for t in (2 * pair, 2 * pair + 1):
+                    rows = slice(t * P, (t + 1) * P)
+                    acc[half, t] = psum.tile([P, HALF], F32, name=f"acc{half}{t}")
+                    nc.tensor.matmul_mx(
+                        out=acc[half, t][:],
+                        lhsT=sr_codes[:, rows].bitcast(FP8X4),
+                        lhsT_scale=sr_scales[:, rows],
+                        rhs=h_codes[:, cols].bitcast(FP8X4),
+                        rhs_scale=h_scales[:, cols],
+                        start=True,
+                        stop=False,
+                    )
 
-        open_groups(0, h_bf0)
-        h_bf1 = keep.tile([P, HALF * PACK], BF16, name="h_bf1", align_bytes=64)
-        weave(nc.scalar.copy, h_bf1, h_rows[:, :, half_cols(1)], 0, HALF)
-        open_groups(1, h_bf1)
-
-        w1_bf0 = keep.tile([P, 2 * N], BF16, name="w1_bf0", tag="h_bf0", align_bytes=64)
+        w1_bf0 = keep.tile([P, 2 * N], BF16, name="w1_bf0", align_bytes=64)
         w1_bf1 = keep.tile([P, 2 * N], BF16, name="w1_bf1", align_bytes=64)
         deal(nc.vector.tensor_copy, w1_bf0[:], w1_raw, 0)
         deal(nc.scalar.copy, w1_bf1[:], w1_raw, 2)
@@ -150,6 +154,7 @@ def tile_picked_ylista_soft_po_kernel(
                     stop=True,
                 )
 
+        nc.scalar.activation(out=neg_thr[:], in_=thr_t[:], func=ACT.Copy, scale=-1.0)
         out_rows = out_0.rearrange("(p t) j -> p t j", t=PACK)
         out_words = out_1[0].rearrange("p n t -> p (n t)").bitcast(I32)
         res = [keep.tile([P, PACK, HALF], F32, name=f"res{half}") for half in range(2)]

@@ -56,7 +56,6 @@ def tile_picked_ylista_soft_po_kernel(
         slot_t = keep.tile([P, S // 16], U16, name="slot_t")
         offs_t = keep.tile([P, S // 16], U16, name="offs_t")
         thr_t = keep.tile([P, PACK], F32, name="thr_t")
-        neg_thr = keep.tile([P, PACK], F32, name="neg_thr")
         mem_t = [keep.tile([P, U], F32, name=f"mem{j}", tag=f"mem{j}", align_bytes=64) for j in range(PACK)]
         sr_raw = keep.tile([P, PACK, N], F32, name="sr_raw")
         w1_raw = keep.tile([P, PACK, N], F32, name="w1_raw")
@@ -154,7 +153,6 @@ def tile_picked_ylista_soft_po_kernel(
                     stop=True,
                 )
 
-        nc.scalar.activation(out=neg_thr[:], in_=thr_t[:], func=ACT.Copy, scale=-1.0)
         out_rows = out_0.rearrange("(p t) j -> p t j", t=PACK)
         out_words = out_1[0].rearrange("p n t -> p (n t)").bitcast(I32)
         res = [keep.tile([P, PACK, HALF], F32, name=f"res{half}") for half in range(2)]
@@ -174,7 +172,7 @@ def tile_picked_ylista_soft_po_kernel(
 
         def clip_below(half, t):
             nc.vector.tensor_scalar(
-                out=up[half][:, t, :], in0=acc[half, t][:], scalar1=neg_thr[:, t : t + 1], scalar2=None, op0=ALU.max
+                out=up[half][:, t, :], in0=acc[half, t][:], scalar1=-1.0, scalar2=thr_t[:, t : t + 1], op0=ALU.mult, op1=ALU.min
             )
 
         def clip_above_and_add(half, t):
@@ -184,11 +182,11 @@ def tile_picked_ylista_soft_po_kernel(
                 scalar=thr_t[:, t : t + 1],
                 in1=up[half][:, t, :],
                 op0=ALU.min,
-                op1=ALU.add,
+                op1=ALU.subtract,
             )
 
-        def store_pair(half, t0):
-            nc.sync.dma_start(out=out_rows[:, t0 : t0 + 2, half_cols(half)], in_=res[half][:, t0 : t0 + 2, :])
+        def store(half, ts):
+            nc.sync.dma_start(out=out_rows[:, ts, half_cols(half)], in_=res[half][:, ts, :])
 
         for half in range(2):
             relus(half, 0)
@@ -196,15 +194,18 @@ def tile_picked_ylista_soft_po_kernel(
             clip_below(half, 3)
             relus(half, 2)
             clip_above_and_add(half, 1)
+            store(half, slice(1, 2))
             subtract(nc.gpsimd, half, 0)
-            store_pair(half, 0)
             clip_above_and_add(half, 3)
             if half == 0:
+                store(half, slice(0, 4, 3))
                 subtract(nc.gpsimd, half, 2)
+                store(half, slice(2, 3))
             else:
+                store(half, slice(3, 4))
                 weave(nc.scalar.copy, res_bf[0], res[0], 0, HALF)
                 subtract(nc.vector, half, 2)
-            store_pair(half, 2)
+                store(half, slice(0, 4, 2))
         weave(nc.vector.tensor_copy, res_bf[1], res[1], LAST_ON_SCALAR, HALF)
         weave(nc.scalar.copy, res_bf[1], res[1], 0, LAST_ON_SCALAR)
 

@@ -22,6 +22,7 @@ LIST_HALF = HALF // 16
 RUN = 4
 SCALE_STEP = P // 16
 LAST_ON_SCALAR = 80
+H_ON_SCALAR = 192
 
 
 def tile_picked_ylista_soft_po_kernel(
@@ -55,11 +56,10 @@ def tile_picked_ylista_soft_po_kernel(
 
         slot_t = keep.tile([P, S // 16], U16, name="slot_t")
         offs_t = keep.tile([P, S // 16], U16, name="offs_t")
-        thr_t = keep.tile([P, PACK], F32, name="thr_t")
         mem_t = [keep.tile([P, U], F32, name=f"mem{j}", tag=f"mem{j}", align_bytes=64) for j in range(PACK)]
         sr_raw = keep.tile([P, PACK, N], F32, name="sr_raw")
         w1_raw = keep.tile([P, PACK, N], F32, name="w1_raw")
-        xs_all = keep.tile([P, T], U8, name="xs_all")
+        xs_all = keep.tile([P, T], U8, name="xs_all", tag="x")
         xw_all = keep.tile([P, T], I32, name="xw_all")
         x_scale = keep.tile([P, S], U8, name="x_scale", align_bytes=64)
 
@@ -75,35 +75,34 @@ def tile_picked_ylista_soft_po_kernel(
         nc.sync.dma_start(out=sr_raw[:], in_=sr.rearrange("(p j) c -> p j c", j=PACK))
         nc.sync.dma_start(out=w1_raw[:], in_=w1.rearrange("(p j) c -> p j c", j=PACK))
         nc.sync.dma_start(out=xw_all[:], in_=x_words[0].rearrange("p n t -> p (n t)").bitcast(I32))
-        nc.sync.dma_start(out=thr_t[:], in_=thr.rearrange("(p t) o -> p (t o)", t=PACK))
 
         h_rows = keep.tile([P, PACK, S], F32, name="h_rows")
         for j in range(3):
             nc.vector.tensor_copy(h_rows[:, j, :], mem_t[j][:].indirect(slot_t[:]))
-        h_bf0 = keep.tile([P, HALF * PACK], BF16, name="h_bf0", align_bytes=64)
-        h_bf1 = keep.tile([P, HALF * PACK], BF16, name="h_bf1", align_bytes=64)
+        h_bf = keep.tile([P, S * PACK], BF16, name="h_bf", align_bytes=64)
         for half in range(2):
             nc.vector.tensor_copy(h_rows[:, 3, half_cols(half)], mem_t[3][:].indirect(list_half(slot_t, half)))
-        weave(scalar_round, h_bf0, h_rows[:, :, half_cols(0)], 0, HALF)
-        nc.gpsimd.tensor_scalar(
-            out=h_bf1[:].rearrange("p (c t) -> p c t", t=PACK),
-            in0=h_rows[:, :, half_cols(1)].rearrange("p t c -> p c t"),
-            scalar1=1.0,
-            scalar2=0.0,
-            op0=ALU.mult,
-            op1=ALU.add,
-        )
+        weave(scalar_round, h_bf, h_rows, 0, H_ON_SCALAR)
+        for c0, c1 in ((H_ON_SCALAR, HALF), (HALF, S)):
+            nc.gpsimd.tensor_scalar(
+                out=h_bf[:, PACK * c0 : PACK * c1].rearrange("p (c t) -> p c t", t=PACK),
+                in0=h_rows[:, :, c0:c1].rearrange("p t c -> p c t"),
+                scalar1=1.0,
+                scalar2=0.0,
+                op0=ALU.mult,
+                op1=ALU.add,
+            )
         xs_picked = keep.tile([P, S], U8, name="xs_picked", align_bytes=64)
         nc.vector.tensor_copy(xs_picked[:], xs_all[:].indirect(offs_t[:]))
         for r in range(4):
             nc.sync.dma_start(
                 out=x_scale[r:P:32, :].bitcast(I32), in_=xs_picked[SCALE_STEP * r : P : 32, :].bitcast(I32)
             )
+        thr_t = keep.tile([P, PACK], F32, name="thr_t", tag="x")
+        nc.sync.dma_start(out=thr_t[:], in_=thr.rearrange("(p t) o -> p (t o)", t=PACK))
         h_codes = keep.tile([P, S], U32, name="h_codes", align_bytes=64)
         h_scales = keep.tile([P, S], U8, name="h_scales", align_bytes=64)
-        for half, h_bf in enumerate((h_bf0, h_bf1)):
-            cols = half_cols(half)
-            nc.vector.quantize_mx(out=h_codes[:, cols].bitcast(FP8X4), scales=h_scales[:, cols], in_=h_bf[:])
+        nc.vector.quantize_mx(out=h_codes[:].bitcast(FP8X4), scales=h_scales[:], in_=h_bf[:])
         sr_codes = keep.tile([P, N], U32, name="sr_codes", align_bytes=64)
         sr_scales = keep.tile([P, N], U8, name="sr_scales", align_bytes=64)
         acc = {}
@@ -197,15 +196,13 @@ def tile_picked_ylista_soft_po_kernel(
             store(half, slice(1, 2))
             subtract(nc.gpsimd, half, 0)
             clip_above_and_add(half, 3)
+            store(half, slice(0, 4, 3))
             if half == 0:
-                store(half, slice(0, 4, 3))
                 subtract(nc.gpsimd, half, 2)
-                store(half, slice(2, 3))
             else:
-                store(half, slice(3, 4))
                 weave(nc.scalar.copy, res_bf[0], res[0], 0, HALF)
                 subtract(nc.vector, half, 2)
-                store(half, slice(0, 4, 2))
+            store(half, slice(2, 3))
         weave(nc.vector.tensor_copy, res_bf[1], res[1], LAST_ON_SCALAR, HALF)
         weave(nc.scalar.copy, res_bf[1], res[1], 0, LAST_ON_SCALAR)
 

@@ -21,7 +21,7 @@ HALF = S // 2
 LIST_HALF = HALF // 16
 RUN = 4
 SCALE_STEP = P // 16
-LAST_ON_SCALAR = 80
+LAST_ON_SCALAR = 64
 H_ON_SCALAR = 192
 
 
@@ -64,7 +64,6 @@ def tile_picked_ylista_soft_po_kernel(
         x_scale = keep.tile([P, S], U8, name="x_scale", align_bytes=64)
 
         nc.vector.memset(xs_all[:].bitcast(I32), 0)
-        nc.vector.memset(x_scale[:].bitcast(I32), 0)
         mem_rows = mem.rearrange("(p j) u -> p j u", j=PACK)
         nc.sync.dma_start(out=mem_t[0][:], in_=mem_rows[:, 0, :])
         nc.sync.dma_start(slot_t[:], slot)
@@ -94,7 +93,8 @@ def tile_picked_ylista_soft_po_kernel(
             )
         xs_picked = keep.tile([P, S], U8, name="xs_picked", align_bytes=64)
         nc.vector.tensor_copy(xs_picked[:], xs_all[:].indirect(offs_t[:]))
-        for r in range(4):
+        nc.vector.tensor_copy(x_scale[:].bitcast(I32), xs_picked[:].bitcast(I32))
+        for r in range(1, 4):
             nc.sync.dma_start(
                 out=x_scale[r:P:32, :].bitcast(I32), in_=xs_picked[SCALE_STEP * r : P : 32, :].bitcast(I32)
             )
@@ -140,7 +140,7 @@ def tile_picked_ylista_soft_po_kernel(
         for half in range(2):
             nc.vector.tensor_copy(x_codes[half][:], xw_all[:].bitcast(U32).indirect(list_half(offs_t, half)))
         for half in range(2):
-            for t in (0, 1, 3, 2):
+            for t in ((0, 1, 3, 2), (0, 2, 3, 1))[half]:
                 rows = slice(t * P, (t + 1) * P)
                 nc.tensor.matmul_mx(
                     out=acc[half, t][:],
@@ -154,61 +154,72 @@ def tile_picked_ylista_soft_po_kernel(
 
         out_rows = out_0.rearrange("(p t) j -> p t j", t=PACK)
         out_words = out_1[0].rearrange("p n t -> p (n t)").bitcast(I32)
-        res = [keep.tile([P, PACK, HALF], F32, name=f"res{half}") for half in range(2)]
-        up = [keep.tile([P, PACK, HALF], F32, name=f"up{half}") for half in range(2)]
-        down = [keep.tile([P, 2, HALF], F32, name=f"down{half}") for half in range(2)]
-        res_bf = [keep.tile([P, HALF * PACK], BF16, name=f"res_bf{half}", align_bytes=64) for half in range(2)]
+        res = keep.tile([P, PACK, S], F32, name="res")
+        up = keep.tile([P, PACK, S], F32, name="up")
+        down = keep.tile([P, PACK, S], F32, name="down")
+        res_bf = keep.tile([P, S * PACK], BF16, name="res_bf", align_bytes=64)
         res_codes = [keep.tile([P, HALF], U32, name=f"res_codes{half}", align_bytes=64) for half in range(2)]
         res_scales = keep.tile([P, S], U8, name="res_scales", align_bytes=64)
 
         def relus(half, t):
-            bias = thr_t[:, t : t + 1]
-            nc.scalar.activation(out=up[half][:, t, :], in_=acc[half, t][:], func=ACT.Relu, bias=bias, scale=1.0)
-            nc.scalar.activation(out=down[half][:, t // 2, :], in_=acc[half, t][:], func=ACT.Relu, bias=bias, scale=-1.0)
+            bias, cols = thr_t[:, t : t + 1], half_cols(half)
+            nc.scalar.activation(out=up[:, t, cols], in_=acc[half, t][:], func=ACT.Relu, bias=bias, scale=1.0)
+            nc.scalar.activation(out=down[:, t, cols], in_=acc[half, t][:], func=ACT.Relu, bias=bias, scale=-1.0)
 
         def subtract(engine, half, t):
-            engine.tensor_tensor(res[half][:, t, :], up[half][:, t, :], down[half][:, t // 2, :], ALU.subtract)
+            cols = half_cols(half)
+            engine.tensor_tensor(res[:, t, cols], up[:, t, cols], down[:, t, cols], ALU.subtract)
 
         def clip_below(half, t):
             nc.vector.tensor_scalar(
-                out=up[half][:, t, :], in0=acc[half, t][:], scalar1=-1.0, scalar2=thr_t[:, t : t + 1], op0=ALU.mult, op1=ALU.min
+                out=up[:, t, half_cols(half)],
+                in0=acc[half, t][:],
+                scalar1=-1.0,
+                scalar2=thr_t[:, t : t + 1],
+                op0=ALU.mult,
+                op1=ALU.min,
             )
 
         def clip_above_and_add(half, t):
             nc.vector.scalar_tensor_tensor(
-                out=res[half][:, t, :],
+                out=res[:, t, half_cols(half)],
                 in0=acc[half, t][:],
                 scalar=thr_t[:, t : t + 1],
-                in1=up[half][:, t, :],
+                in1=up[:, t, half_cols(half)],
                 op0=ALU.min,
                 op1=ALU.subtract,
             )
 
-        def store(half, ts):
-            nc.sync.dma_start(out=out_rows[:, ts, half_cols(half)], in_=res[half][:, ts, :])
+        def store(ts, cols):
+            nc.sync.dma_start(out=out_rows[:, ts, cols], in_=res[:, ts, cols])
 
-        for half in range(2):
-            relus(half, 0)
-            clip_below(half, 1)
-            clip_below(half, 3)
-            relus(half, 2)
-            clip_above_and_add(half, 1)
-            store(half, slice(1, 2))
-            subtract(nc.gpsimd, half, 0)
-            clip_above_and_add(half, 3)
-            store(half, slice(0, 4, 3))
-            if half == 0:
-                subtract(nc.gpsimd, half, 2)
-            else:
-                weave(nc.scalar.copy, res_bf[0], res[0], 0, HALF)
-                subtract(nc.vector, half, 2)
-            store(half, slice(2, 3))
-        weave(nc.vector.tensor_copy, res_bf[1], res[1], LAST_ON_SCALAR, HALF)
-        weave(nc.scalar.copy, res_bf[1], res[1], 0, LAST_ON_SCALAR)
+        relus(0, 0)
+        clip_below(0, 1)
+        clip_below(0, 3)
+        relus(0, 2)
+        clip_above_and_add(0, 1)
+        subtract(nc.gpsimd, 0, 0)
+        store(slice(0, 2), half_cols(0))
+        clip_above_and_add(0, 3)
+        subtract(nc.gpsimd, 0, 2)
+        relus(1, 0)
+        clip_below(1, 2)
+        clip_below(1, 3)
+        relus(1, 1)
+        clip_above_and_add(1, 2)
+        store(slice(2, 3), slice(0, S))
+        subtract(nc.gpsimd, 1, 0)
+        clip_above_and_add(1, 3)
+        store(slice(3, 4), slice(0, S))
+        weave(nc.scalar.copy, res_bf, res, 0, HALF)
+        subtract(nc.vector, 1, 1)
+        store(slice(0, 2), half_cols(1))
+        weave(nc.vector.tensor_copy, res_bf, res, HALF + LAST_ON_SCALAR, S)
+        weave(nc.scalar.copy, res_bf, res, HALF, HALF + LAST_ON_SCALAR)
 
         for half in range(2):
             cols = half_cols(half)
-            nc.vector.quantize_mx(out=res_codes[half][:].bitcast(FP8X4), scales=res_scales[:, cols], in_=res_bf[half][:])
+            nc.vector.quantize_mx(out=res_codes[half][:].bitcast(FP8X4), scales=res_scales[:, cols], in_=res_bf[:, PACK * half * HALF : PACK * (half + 1) * HALF])
             nc.sync.dma_start(out=out_words[:, cols], in_=res_codes[half][:].bitcast(I32))
         for q in range(4):
             queue = nc.scalar if q % 2 == 0 else nc.sync

@@ -21,7 +21,8 @@ HALF = S // 2
 LIST_HALF = HALF // 16
 RUN = 4
 SCALE_STEP = P // 16
-LAST_ON_SCALAR = 64
+FIRST_ON_SCALAR = 192
+LAST_ON_SCALAR = 96
 H_ON_SCALAR = 192
 
 
@@ -140,7 +141,7 @@ def tile_picked_ylista_soft_po_kernel(
         for half in range(2):
             nc.vector.tensor_copy(x_codes[half][:], xw_all[:].bitcast(U32).indirect(list_half(offs_t, half)))
         for half in range(2):
-            for t in ((0, 1, 3, 2), (0, 2, 3, 1))[half]:
+            for t in ((0, 1, 2, 3), (0, 2, 1, 3))[half]:
                 rows = slice(t * P, (t + 1) * P)
                 nc.tensor.matmul_mx(
                     out=acc[half, t][:],
@@ -157,6 +158,7 @@ def tile_picked_ylista_soft_po_kernel(
         res = keep.tile([P, PACK, S], F32, name="res")
         up = keep.tile([P, PACK, S], F32, name="up")
         down = keep.tile([P, PACK, S], F32, name="down")
+        low = keep.tile([P, PACK, HALF], F32, name="low")
         res_bf = keep.tile([P, S * PACK], BF16, name="res_bf", align_bytes=64)
         res_codes = [keep.tile([P, HALF], U32, name=f"res_codes{half}", align_bytes=64) for half in range(2)]
         res_scales = keep.tile([P, S], U8, name="res_scales", align_bytes=64)
@@ -172,7 +174,7 @@ def tile_picked_ylista_soft_po_kernel(
 
         def clip_below(half, t):
             nc.vector.tensor_scalar(
-                out=up[:, t, half_cols(half)],
+                out=low[:, t, :],
                 in0=acc[half, t][:],
                 scalar1=-1.0,
                 scalar2=thr_t[:, t : t + 1],
@@ -185,7 +187,7 @@ def tile_picked_ylista_soft_po_kernel(
                 out=res[:, t, half_cols(half)],
                 in0=acc[half, t][:],
                 scalar=thr_t[:, t : t + 1],
-                in1=up[:, t, half_cols(half)],
+                in1=low[:, t, :],
                 op0=ALU.min,
                 op1=ALU.subtract,
             )
@@ -194,26 +196,26 @@ def tile_picked_ylista_soft_po_kernel(
             nc.sync.dma_start(out=out_rows[:, ts, cols], in_=res[:, ts, cols])
 
         relus(0, 0)
-        clip_below(0, 1)
-        clip_below(0, 3)
-        relus(0, 2)
-        clip_above_and_add(0, 1)
+        for t in (1, 2, 3):
+            clip_below(0, t)
         subtract(nc.gpsimd, 0, 0)
-        store(slice(0, 2), half_cols(0))
-        clip_above_and_add(0, 3)
-        subtract(nc.gpsimd, 0, 2)
         relus(1, 0)
-        clip_below(1, 2)
-        clip_below(1, 3)
-        relus(1, 1)
-        clip_above_and_add(1, 2)
-        store(slice(2, 3), slice(0, S))
+        clip_above_and_add(0, 1)
+        store(slice(0, 2), half_cols(0))
+        clip_above_and_add(0, 2)
+        clip_above_and_add(0, 3)
+        store(slice(2, 4), half_cols(0))
         subtract(nc.gpsimd, 1, 0)
-        clip_above_and_add(1, 3)
-        store(slice(3, 4), slice(0, S))
-        weave(nc.scalar.copy, res_bf, res, 0, HALF)
-        subtract(nc.vector, 1, 1)
+        relus(1, 2)
+        clip_below(1, 1)
+        weave(nc.vector.tensor_copy, res_bf, res, FIRST_ON_SCALAR, HALF)
+        clip_above_and_add(1, 1)
         store(slice(0, 2), half_cols(1))
+        subtract(nc.gpsimd, 1, 2)
+        relus(1, 3)
+        weave(nc.scalar.copy, res_bf, res, 0, FIRST_ON_SCALAR)
+        subtract(nc.vector, 1, 3)
+        store(slice(2, 4), half_cols(1))
         weave(nc.vector.tensor_copy, res_bf, res, HALF + LAST_ON_SCALAR, S)
         weave(nc.scalar.copy, res_bf, res, HALF, HALF + LAST_ON_SCALAR)
 

@@ -141,7 +141,7 @@ def tile_picked_ylista_soft_po_kernel(
         for half in range(2):
             nc.vector.tensor_copy(x_codes[half][:], xw_all[:].bitcast(U32).indirect(list_half(offs_t, half)))
         for half in range(2):
-            for t in ((0, 1, 2, 3), (0, 2, 1, 3))[half]:
+            for t in ((2, 0, 1, 3), (0, 2, 3, 1))[half]:
                 rows = slice(t * P, (t + 1) * P)
                 nc.tensor.matmul_mx(
                     out=acc[half, t][:],
@@ -158,8 +158,9 @@ def tile_picked_ylista_soft_po_kernel(
         res = keep.tile([P, PACK, S], F32, name="res")
         up = keep.tile([P, PACK, S], F32, name="up")
         down = keep.tile([P, PACK, S], F32, name="down")
-        low = keep.tile([P, PACK, HALF], F32, name="low")
         res_bf = keep.tile([P, S * PACK], BF16, name="res_bf", align_bytes=64)
+        low_even = keep.tile([P, HALF], F32, name="low_even")
+        low = (low_even[:], res_bf[:, PACK * FIRST_ON_SCALAR : PACK * FIRST_ON_SCALAR + 2 * HALF].bitcast(F32))
         res_codes = [keep.tile([P, HALF], U32, name=f"res_codes{half}", align_bytes=64) for half in range(2)]
         res_scales = keep.tile([P, S], U8, name="res_scales", align_bytes=64)
 
@@ -174,7 +175,7 @@ def tile_picked_ylista_soft_po_kernel(
 
         def clip_below(half, t):
             nc.vector.tensor_scalar(
-                out=low[:, t, :],
+                out=low[t % 2],
                 in0=acc[half, t][:],
                 scalar1=-1.0,
                 scalar2=thr_t[:, t : t + 1],
@@ -187,7 +188,7 @@ def tile_picked_ylista_soft_po_kernel(
                 out=res[:, t, half_cols(half)],
                 in0=acc[half, t][:],
                 scalar=thr_t[:, t : t + 1],
-                in1=low[:, t, :],
+                in1=low[t % 2],
                 op0=ALU.min,
                 op1=ALU.subtract,
             )
@@ -195,27 +196,28 @@ def tile_picked_ylista_soft_po_kernel(
         def store(ts, cols):
             nc.sync.dma_start(out=out_rows[:, ts, cols], in_=res[:, ts, cols])
 
-        relus(0, 0)
-        for t in (1, 2, 3):
-            clip_below(0, t)
-        subtract(nc.gpsimd, 0, 0)
-        relus(1, 0)
+        relus(0, 2)
+        clip_below(0, 0)
+        clip_below(0, 1)
+        subtract(nc.gpsimd, 0, 2)
+        relus(0, 3)
+        clip_above_and_add(0, 0)
         clip_above_and_add(0, 1)
         store(slice(0, 2), half_cols(0))
-        clip_above_and_add(0, 2)
-        clip_above_and_add(0, 3)
-        store(slice(2, 4), half_cols(0))
+        subtract(nc.gpsimd, 0, 3)
+        relus(1, 0)
+        clip_below(1, 2)
+        clip_below(1, 3)
+        clip_above_and_add(1, 2)
+        store(slice(2, 3), slice(0, S))
         subtract(nc.gpsimd, 1, 0)
-        relus(1, 2)
-        clip_below(1, 1)
-        weave(nc.vector.tensor_copy, res_bf, res, FIRST_ON_SCALAR, HALF)
-        clip_above_and_add(1, 1)
-        store(slice(0, 2), half_cols(1))
-        subtract(nc.gpsimd, 1, 2)
-        relus(1, 3)
+        relus(1, 1)
+        clip_above_and_add(1, 3)
+        store(slice(3, 4), slice(0, S))
         weave(nc.scalar.copy, res_bf, res, 0, FIRST_ON_SCALAR)
-        subtract(nc.vector, 1, 3)
-        store(slice(2, 4), half_cols(1))
+        weave(nc.vector.tensor_copy, res_bf, res, FIRST_ON_SCALAR, HALF)
+        subtract(nc.vector, 1, 1)
+        store(slice(0, 2), half_cols(1))
         weave(nc.vector.tensor_copy, res_bf, res, HALF + LAST_ON_SCALAR, S)
         weave(nc.scalar.copy, res_bf, res, HALF, HALF + LAST_ON_SCALAR)
 

@@ -210,13 +210,14 @@ def tile_picked_ylista_soft_po_kernel(
         clip_below(1, 3)
         clip_above_and_add(1, 2)
         store(slice(2, 3), slice(0, S))
-        subtract(nc.gpsimd, 1, 0)
         relus(1, 1)
         clip_above_and_add(1, 3)
         store(slice(3, 4), slice(0, S))
         weave(nc.scalar.copy, res_bf, res, 0, FIRST_ON_SCALAR)
         weave(nc.vector.tensor_copy, res_bf, res, FIRST_ON_SCALAR, HALF)
-        subtract(nc.vector, 1, 1)
+        nc.vector.tensor_tensor(
+            res[:, 0:2, half_cols(1)], up[:, 0:2, half_cols(1)], down[:, 0:2, half_cols(1)], ALU.subtract
+        )
         store(slice(0, 2), half_cols(1))
         weave(nc.vector.tensor_copy, res_bf, res, HALF + LAST_ON_SCALAR, S)
         weave(nc.scalar.copy, res_bf, res, HALF, HALF + LAST_ON_SCALAR)

@@ -17,6 +17,7 @@ ACT = mybir.ActivationFunctionType
 
 P = 128
 PACK = 4
+ALIGN = 256
 HALF = S // 2
 LIST_HALF = HALF // 16
 RUN = 4
@@ -55,33 +56,36 @@ def tile_picked_ylista_soft_po_kernel(
                 in_=raw[:].rearrange("p j (m t) -> p m j t", t=PACK)[:, :, :, t0 : t0 + 2],
             )
 
-        slot_t = keep.tile([P, S // 16], U16, name="slot_t")
-        offs_t = keep.tile([P, S // 16], U16, name="offs_t")
-        mem_t = [keep.tile([P, U], F32, name=f"mem{j}", tag=f"mem{j}", align_bytes=64) for j in range(PACK)]
-        sr_raw = keep.tile([P, PACK, N], F32, name="sr_raw")
-        w1_raw = keep.tile([P, PACK, N], F32, name="w1_raw")
-        xs_all = keep.tile([P, T], U8, name="xs_all", tag="x")
-        xw_all = keep.tile([P, T], I32, name="xw_all")
-        x_scale = keep.tile([P, S], U8, name="x_scale", align_bytes=64)
+        slot_t = keep.tile([P, S // 16], U16, name="slot_t", align_bytes=ALIGN)
+        offs_t = keep.tile([P, S // 16], U16, name="offs_t", align_bytes=ALIGN)
+        mem_low = keep.tile([P, 2, U], F32, name="mem_low", align_bytes=ALIGN)
+        mem_high = [keep.tile([P, U], F32, name=f"mem{j}", align_bytes=ALIGN) for j in (2, 3)]
+        mem_t = [mem_low[:, 0, :], mem_low[:, 1, :], mem_high[0][:], mem_high[1][:]]
+        sr_raw = keep.tile([P, PACK, N], F32, name="sr_raw", align_bytes=ALIGN)
+        w1_raw = keep.tile([P, PACK, N], F32, name="w1_raw", align_bytes=ALIGN)
+        xs_all = keep.tile([P, T], U8, name="xs_all", tag="x", align_bytes=ALIGN)
+        xw_all = keep.tile([P, T], I32, name="xw_all", align_bytes=ALIGN)
+        x_scale = keep.tile([P, S], U8, name="x_scale", align_bytes=ALIGN)
 
         nc.vector.memset(xs_all[:].bitcast(I32), 0)
         mem_rows = mem.rearrange("(p j) u -> p j u", j=PACK)
-        nc.sync.dma_start(out=mem_t[0][:], in_=mem_rows[:, 0, :])
+        nc.sync.dma_start(out=mem_low[:], in_=mem_rows[:, 0:2, :])
         nc.sync.dma_start(slot_t[:], slot)
-        for j in range(1, PACK):
-            nc.sync.dma_start(out=mem_t[j][:], in_=mem_rows[:, j, :])
+        for j in (2, 3):
+            nc.sync.dma_start(out=mem_t[j], in_=mem_rows[:, j, :])
         nc.sync.dma_start(offs_t[:], offs)
         nc.sync.dma_start(out=xs_all[0:P:SCALE_STEP, :].bitcast(I32), in_=x_scales[0].bitcast(I32))
         nc.sync.dma_start(out=sr_raw[:], in_=sr.rearrange("(p j) c -> p j c", j=PACK))
         nc.sync.dma_start(out=w1_raw[:], in_=w1.rearrange("(p j) c -> p j c", j=PACK))
         nc.sync.dma_start(out=xw_all[:], in_=x_words[0].rearrange("p n t -> p (n t)").bitcast(I32))
 
-        h_rows = keep.tile([P, PACK, S], F32, name="h_rows")
-        for j in range(3):
-            nc.vector.tensor_copy(h_rows[:, j, :], mem_t[j][:].indirect(slot_t[:]))
-        h_bf = keep.tile([P, S * PACK], BF16, name="h_bf", align_bytes=64)
+        h_rows = keep.tile([P, PACK, S], F32, name="h_rows", align_bytes=ALIGN)
+        for j in (0, 2):
+            nc.vector.tensor_copy(h_rows[:, j, :], mem_t[j].indirect(slot_t[:]))
+        scalar_round(h_rows[:, 1, :], mem_t[1].indirect(slot_t[:]))
+        h_bf = keep.tile([P, S * PACK], BF16, name="h_bf", align_bytes=ALIGN)
         for half in range(2):
-            nc.vector.tensor_copy(h_rows[:, 3, half_cols(half)], mem_t[3][:].indirect(list_half(slot_t, half)))
+            nc.vector.tensor_copy(h_rows[:, 3, half_cols(half)], mem_t[3].indirect(list_half(slot_t, half)))
         weave(scalar_round, h_bf, h_rows, 0, H_ON_SCALAR)
         for c0, c1 in ((H_ON_SCALAR, HALF), (HALF, S)):
             nc.gpsimd.tensor_scalar(
@@ -92,23 +96,23 @@ def tile_picked_ylista_soft_po_kernel(
                 op0=ALU.mult,
                 op1=ALU.add,
             )
-        xs_picked = keep.tile([P, S], U8, name="xs_picked", align_bytes=64)
+        xs_picked = keep.tile([P, S], U8, name="xs_picked", align_bytes=ALIGN)
         nc.vector.tensor_copy(xs_picked[:], xs_all[:].indirect(offs_t[:]))
         nc.vector.tensor_copy(x_scale[:].bitcast(I32), xs_picked[:].bitcast(I32))
         for r in range(1, 4):
             nc.sync.dma_start(
                 out=x_scale[r:P:32, :].bitcast(I32), in_=xs_picked[SCALE_STEP * r : P : 32, :].bitcast(I32)
             )
-        thr_t = keep.tile([P, PACK], F32, name="thr_t", tag="x")
+        thr_t = keep.tile([P, PACK], F32, name="thr_t", tag="x", align_bytes=ALIGN)
         nc.sync.dma_start(out=thr_t[:], in_=thr.rearrange("(p t) o -> p (t o)", t=PACK))
-        h_codes = keep.tile([P, S], U32, name="h_codes", align_bytes=64)
-        h_scales = keep.tile([P, S], U8, name="h_scales", align_bytes=64)
+        h_codes = keep.tile([P, S], U32, name="h_codes", align_bytes=ALIGN)
+        h_scales = keep.tile([P, S], U8, name="h_scales", align_bytes=ALIGN)
         nc.vector.quantize_mx(out=h_codes[:].bitcast(FP8X4), scales=h_scales[:], in_=h_bf[:])
-        sr_codes = keep.tile([P, N], U32, name="sr_codes", align_bytes=64)
-        sr_scales = keep.tile([P, N], U8, name="sr_scales", align_bytes=64)
+        sr_codes = keep.tile([P, N], U32, name="sr_codes", align_bytes=ALIGN)
+        sr_scales = keep.tile([P, N], U8, name="sr_scales", align_bytes=ALIGN)
         acc = {}
         for pair in range(2):
-            sr_bf = keep.tile([P, 2 * N], BF16, name=f"sr_bf{pair}", align_bytes=64)
+            sr_bf = keep.tile([P, 2 * N], BF16, name=f"sr_bf{pair}", align_bytes=ALIGN)
             deal(nc.scalar.copy, sr_bf[:], sr_raw, 2 * pair)
             rows = slice(pair * 2 * P, (pair + 1) * 2 * P)
             nc.vector.quantize_mx(out=sr_codes[:, rows].bitcast(FP8X4), scales=sr_scales[:, rows], in_=sr_bf[:])
@@ -127,17 +131,17 @@ def tile_picked_ylista_soft_po_kernel(
                         stop=False,
                     )
 
-        w1_bf0 = keep.tile([P, 2 * N], BF16, name="w1_bf0", align_bytes=64)
-        w1_bf1 = keep.tile([P, 2 * N], BF16, name="w1_bf1", align_bytes=64)
+        w1_bf0 = keep.tile([P, 2 * N], BF16, name="w1_bf0", align_bytes=ALIGN)
+        w1_bf1 = keep.tile([P, 2 * N], BF16, name="w1_bf1", align_bytes=ALIGN)
         deal(nc.vector.tensor_copy, w1_bf0[:], w1_raw, 0)
         deal(nc.scalar.copy, w1_bf1[:], w1_raw, 2)
-        w1_codes = keep.tile([P, N], U32, name="w1_codes", align_bytes=64)
-        w1_scales = keep.tile([P, N], U8, name="w1_scales", align_bytes=64)
+        w1_codes = keep.tile([P, N], U32, name="w1_codes", align_bytes=ALIGN)
+        w1_scales = keep.tile([P, N], U8, name="w1_scales", align_bytes=ALIGN)
         for pair, w1_bf in enumerate((w1_bf0, w1_bf1)):
             rows = slice(pair * 2 * P, (pair + 1) * 2 * P)
             nc.vector.quantize_mx(out=w1_codes[:, rows].bitcast(FP8X4), scales=w1_scales[:, rows], in_=w1_bf[:])
 
-        x_codes = [keep.tile([P, HALF], U32, name=f"x_codes{half}", align_bytes=64) for half in range(2)]
+        x_codes = [keep.tile([P, HALF], U32, name=f"x_codes{half}", align_bytes=ALIGN) for half in range(2)]
         for half in range(2):
             nc.vector.tensor_copy(x_codes[half][:], xw_all[:].bitcast(U32).indirect(list_half(offs_t, half)))
         for half in range(2):
@@ -155,14 +159,14 @@ def tile_picked_ylista_soft_po_kernel(
 
         out_rows = out_0.rearrange("(p t) j -> p t j", t=PACK)
         out_words = out_1[0].rearrange("p n t -> p (n t)").bitcast(I32)
-        res = keep.tile([P, PACK, S], F32, name="res")
-        up = keep.tile([P, PACK, S], F32, name="up")
-        down = keep.tile([P, PACK, S], F32, name="down")
-        res_bf = keep.tile([P, S * PACK], BF16, name="res_bf", align_bytes=64)
-        low_even = keep.tile([P, HALF], F32, name="low_even")
+        res = keep.tile([P, PACK, S], F32, name="res", align_bytes=ALIGN)
+        up = keep.tile([P, PACK, S], F32, name="up", align_bytes=ALIGN)
+        down = keep.tile([P, PACK, S], F32, name="down", align_bytes=ALIGN)
+        res_bf = keep.tile([P, S * PACK], BF16, name="res_bf", align_bytes=ALIGN)
+        low_even = keep.tile([P, HALF], F32, name="low_even", align_bytes=ALIGN)
         low = (low_even[:], res_bf[:, PACK * FIRST_ON_SCALAR : PACK * FIRST_ON_SCALAR + 2 * HALF].bitcast(F32))
-        res_codes = [keep.tile([P, HALF], U32, name=f"res_codes{half}", align_bytes=64) for half in range(2)]
-        res_scales = keep.tile([P, S], U8, name="res_scales", align_bytes=64)
+        res_codes = [keep.tile([P, HALF], U32, name=f"res_codes{half}", align_bytes=ALIGN) for half in range(2)]
+        res_scales = keep.tile([P, S], U8, name="res_scales", align_bytes=ALIGN)
 
         def relus(half, t):
             bias, cols = thr_t[:, t : t + 1], half_cols(half)
@@ -202,8 +206,9 @@ def tile_picked_ylista_soft_po_kernel(
         subtract(nc.gpsimd, 0, 2)
         relus(0, 3)
         clip_above_and_add(0, 0)
+        store(slice(0, 1), half_cols(0))
         clip_above_and_add(0, 1)
-        store(slice(0, 2), half_cols(0))
+        store(slice(1, 2), half_cols(0))
         subtract(nc.gpsimd, 0, 3)
         relus(1, 0)
         clip_below(1, 2)

from contextlib import ExitStack

import concourse.mybir as mybir

K, T, S, H, N, U = 512, 2048, 512, 512, 512, 1024
FLOPS = 2 * N * S * (K + H)

F32 = mybir.dt.float32
BF16 = mybir.dt.bfloat16
I32 = mybir.dt.int32
U32 = mybir.dt.uint32
U16 = mybir.dt.uint16
U8 = mybir.dt.uint8
FP8X4 = mybir.dt.float8_e4m3fn_x4
ALU = mybir.AluOpType
ACT = mybir.ActivationFunctionType

P = 128
PACK = 4
ALIGN = 256
HALF = S // 2
LIST_HALF = HALF // 16
RUN = 4
SCALE_STEP = P // 16
FIRST_ON_SCALAR = 192
LAST_ON_SCALAR = 96
H_ON_SCALAR = 192


def tile_picked_ylista_soft_po_kernel(
    tc, x_words, x_scales, mem, w1, sr, thr, offs, slot, out_0, out_1, out_2
):
    nc = tc.nc
    with ExitStack() as ctx:
        keep = ctx.enter_context(tc.tile_pool(name="keep", bufs=1))
        psum = ctx.enter_context(tc.psum_pool(name="psum", bufs=1))

        def half_cols(half):
            return slice(half * HALF, (half + 1) * HALF)

        def list_half(tile, half):
            return tile[:, half * LIST_HALF : (half + 1) * LIST_HALF]

        def scalar_round(out, in_):
            nc.scalar.activation(out=out, in_=in_, func=ACT.Copy)

        def weave(copy, dst, src, c0, c1):
            copy(
                out=dst[:, PACK * c0 : PACK * c1].rearrange("p (c i t) -> p c t i", i=RUN, t=PACK),
                in_=src[:, :, c0:c1].rearrange("p t (c i) -> p c t i", i=RUN),
            )

        def deal(copy, dst, raw, t0):
            copy(
                out=dst.rearrange("p (t m j) -> p m j t", t=2, j=PACK),
                in_=raw[:].rearrange("p j (m t) -> p m j t", t=PACK)[:, :, :, t0 : t0 + 2],
            )

        slot_t = keep.tile([P, S // 16], U16, name="slot_t", align_bytes=ALIGN)
        offs_t = keep.tile([P, S // 16], U16, name="offs_t", align_bytes=ALIGN)
        mem_low = keep.tile([P, 2, U], F32, name="mem_low", align_bytes=ALIGN)
        mem_high = [keep.tile([P, U], F32, name=f"mem{j}", align_bytes=ALIGN) for j in (2, 3)]
        mem_t = [mem_low[:, 0, :], mem_low[:, 1, :], mem_high[0][:], mem_high[1][:]]
        sr_raw = keep.tile([P, PACK, N], F32, name="sr_raw", align_bytes=ALIGN)
        w1_raw = keep.tile([P, PACK, N], F32, name="w1_raw", align_bytes=ALIGN)
        xs_all = keep.tile([P, T], U8, name="xs_all", tag="x", align_bytes=ALIGN)
        xw_all = keep.tile([P, T], I32, name="xw_all", align_bytes=ALIGN)
        x_scale = keep.tile([P, S], U8, name="x_scale", align_bytes=ALIGN)

        nc.vector.memset(xs_all[:].bitcast(I32), 0)
        mem_rows = mem.rearrange("(p j) u -> p j u", j=PACK)
        nc.sync.dma_start(out=mem_low[:], in_=mem_rows[:, 0:2, :])
        nc.sync.dma_start(slot_t[:], slot)
        for j in (2, 3):
            nc.sync.dma_start(out=mem_t[j], in_=mem_rows[:, j, :])
        nc.sync.dma_start(offs_t[:], offs)
        nc.sync.dma_start(out=xs_all[0:P:SCALE_STEP, :].bitcast(I32), in_=x_scales[0].bitcast(I32))
        nc.sync.dma_start(out=sr_raw[:], in_=sr.rearrange("(p j) c -> p j c", j=PACK))
        nc.sync.dma_start(out=w1_raw[:], in_=w1.rearrange("(p j) c -> p j c", j=PACK))
        nc.sync.dma_start(out=xw_all[:], in_=x_words[0].rearrange("p n t -> p (n t)").bitcast(I32))

        h_rows = keep.tile([P, PACK, S], F32, name="h_rows", align_bytes=ALIGN)
        for j in (0, 2):
            nc.vector.tensor_copy(h_rows[:, j, :], mem_t[j].indirect(slot_t[:]))
        scalar_round(h_rows[:, 1, :], mem_t[1].indirect(slot_t[:]))
        h_bf = keep.tile([P, S * PACK], BF16, name="h_bf", align_bytes=ALIGN)
        for half in range(2):
            nc.vector.tensor_copy(h_rows[:, 3, half_cols(half)], mem_t[3].indirect(list_half(slot_t, half)))
        weave(scalar_round, h_bf, h_rows, 0, H_ON_SCALAR)
        for c0, c1 in ((H_ON_SCALAR, HALF), (HALF, S)):
            nc.gpsimd.tensor_scalar(
                out=h_bf[:, PACK * c0 : PACK * c1].rearrange("p (c t) -> p c t", t=PACK),
                in0=h_rows[:, :, c0:c1].rearrange("p t c -> p c t"),
                scalar1=1.0,
                scalar2=0.0,
                op0=ALU.mult,
                op1=ALU.add,
            )
        xs_picked = keep.tile([P, S], U8, name="xs_picked", align_bytes=ALIGN)
        nc.vector.tensor_copy(xs_picked[:], xs_all[:].indirect(offs_t[:]))
        nc.vector.tensor_copy(x_scale[:].bitcast(I32), xs_picked[:].bitcast(I32))
        for r in range(1, 4):
            nc.sync.dma_start(
                out=x_scale[r:P:32, :].bitcast(I32), in_=xs_picked[SCALE_STEP * r : P : 32, :].bitcast(I32)
            )
        thr_t = keep.tile([P, PACK], F32, name="thr_t", tag="x", align_bytes=ALIGN)
        nc.sync.dma_start(out=thr_t[:], in_=thr.rearrange("(p t) o -> p (t o)", t=PACK))
        h_codes = keep.tile([P, S], U32, name="h_codes", align_bytes=ALIGN)
        h_scales = keep.tile([P, S], U8, name="h_scales", align_bytes=ALIGN)
        nc.vector.quantize_mx(out=h_codes[:].bitcast(FP8X4), scales=h_scales[:], in_=h_bf[:])
        sr_codes = keep.tile([P, N], U32, name="sr_codes", align_bytes=ALIGN)
        sr_scales = keep.tile([P, N], U8, name="sr_scales", align_bytes=ALIGN)
        acc = {}
        for pair in range(2):
            sr_bf = keep.tile([P, 2 * N], BF16, name=f"sr_bf{pair}", align_bytes=ALIGN)
            deal(nc.scalar.copy, sr_bf[:], sr_raw, 2 * pair)
            rows = slice(pair * 2 * P, (pair + 1) * 2 * P)
            nc.vector.quantize_mx(out=sr_codes[:, rows].bitcast(FP8X4), scales=sr_scales[:, rows], in_=sr_bf[:])
            for half in range(2):
                cols = half_cols(half)
                for t in (2 * pair, 2 * pair + 1):
                    rows = slice(t * P, (t + 1) * P)
                    acc[half, t] = psum.tile([P, HALF], F32, name=f"acc{half}{t}")
                    nc.tensor.matmul_mx(
                        out=acc[half, t][:],
                        lhsT=sr_codes[:, rows].bitcast(FP8X4),
                        lhsT_scale=sr_scales[:, rows],
                        rhs=h_codes[:, cols].bitcast(FP8X4),
                        rhs_scale=h_scales[:, cols],
                        start=True,
                        stop=False,
                    )

        w1_bf0 = keep.tile([P, 2 * N], BF16, name="w1_bf0", align_bytes=ALIGN)
        w1_bf1 = keep.tile([P, 2 * N], BF16, name="w1_bf1", align_bytes=ALIGN)
        deal(nc.vector.tensor_copy, w1_bf0[:], w1_raw, 0)
        deal(nc.scalar.copy, w1_bf1[:], w1_raw, 2)
        w1_codes = keep.tile([P, N], U32, name="w1_codes", align_bytes=ALIGN)
        w1_scales = keep.tile([P, N], U8, name="w1_scales", align_bytes=ALIGN)
        for pair, w1_bf in enumerate((w1_bf0, w1_bf1)):
            rows = slice(pair * 2 * P, (pair + 1) * 2 * P)
            nc.vector.quantize_mx(out=w1_codes[:, rows].bitcast(FP8X4), scales=w1_scales[:, rows], in_=w1_bf[:])

        x_codes = [keep.tile([P, HALF], U32, name=f"x_codes{half}", align_bytes=ALIGN) for half in range(2)]
        for half in range(2):
            nc.vector.tensor_copy(x_codes[half][:], xw_all[:].bitcast(U32).indirect(list_half(offs_t, half)))
        for half in range(2):
            for t in ((2, 0, 1, 3), (0, 2, 3, 1))[half]:
                rows = slice(t * P, (t + 1) * P)
                nc.tensor.matmul_mx(
                    out=acc[half, t][:],
                    lhsT=w1_codes[:, rows].bitcast(FP8X4),
                    lhsT_scale=w1_scales[:, rows],
                    rhs=x_codes[half][:].bitcast(FP8X4),
                    rhs_scale=x_scale[:, half_cols(half)],
                    start=False,
                    stop=True,
                )

        out_rows = out_0.rearrange("(p t) j -> p t j", t=PACK)
        out_words = out_1[0].rearrange("p n t -> p (n t)").bitcast(I32)
        res = keep.tile([P, PACK, S], F32, name="res", align_bytes=ALIGN)
        up = keep.tile([P, PACK, S], F32, name="up", align_bytes=ALIGN)
        down = keep.tile([P, PACK, S], F32, name="down", align_bytes=ALIGN)
        res_bf = keep.tile([P, S * PACK], BF16, name="res_bf", align_bytes=ALIGN)
        low_even = keep.tile([P, HALF], F32, name="low_even", align_bytes=ALIGN)
        low = (low_even[:], res_bf[:, PACK * FIRST_ON_SCALAR : PACK * FIRST_ON_SCALAR + 2 * HALF].bitcast(F32))
        res_codes = [keep.tile([P, HALF], U32, name=f"res_codes{half}", align_bytes=ALIGN) for half in range(2)]
        res_scales = keep.tile([P, S], U8, name="res_scales", align_bytes=ALIGN)

        def relus(half, t):
            bias, cols = thr_t[:, t : t + 1], half_cols(half)
            nc.scalar.activation(out=up[:, t, cols], in_=acc[half, t][:], func=ACT.Relu, bias=bias, scale=1.0)
            nc.scalar.activation(out=down[:, t, cols], in_=acc[half, t][:], func=ACT.Relu, bias=bias, scale=-1.0)

        def subtract(engine, half, t):
            cols = half_cols(half)
            engine.tensor_tensor(res[:, t, cols], up[:, t, cols], down[:, t, cols], ALU.subtract)

        def clip_below(half, t):
            nc.vector.tensor_scalar(
                out=low[t % 2],
                in0=acc[half, t][:],
                scalar1=-1.0,
                scalar2=thr_t[:, t : t + 1],
                op0=ALU.mult,
                op1=ALU.min,
            )

        def clip_above_and_add(half, t):
            nc.vector.scalar_tensor_tensor(
                out=res[:, t, half_cols(half)],
                in0=acc[half, t][:],
                scalar=thr_t[:, t : t + 1],
                in1=low[t % 2],
                op0=ALU.min,
                op1=ALU.subtract,
            )

        def store(ts, cols):
            nc.sync.dma_start(out=out_rows[:, ts, cols], in_=res[:, ts, cols])

        relus(0, 2)
        clip_below(0, 0)
        clip_below(0, 1)
        subtract(nc.gpsimd, 0, 2)
        relus(0, 3)
        clip_above_and_add(0, 0)
        store(slice(0, 1), half_cols(0))
        clip_above_and_add(0, 1)
        store(slice(1, 2), half_cols(0))
        subtract(nc.gpsimd, 0, 3)
        relus(1, 0)
        clip_below(1, 2)
        clip_below(1, 3)
        clip_above_and_add(1, 2)
        store(slice(2, 3), slice(0, S))
        relus(1, 1)
        clip_above_and_add(1, 3)
        store(slice(3, 4), slice(0, S))
        weave(nc.scalar.copy, res_bf, res, 0, FIRST_ON_SCALAR)
        weave(nc.vector.tensor_copy, res_bf, res, FIRST_ON_SCALAR, HALF)
        nc.vector.tensor_tensor(
            res[:, 0:2, half_cols(1)], up[:, 0:2, half_cols(1)], down[:, 0:2, half_cols(1)], ALU.subtract
        )
        store(slice(0, 2), half_cols(1))
        weave(nc.vector.tensor_copy, res_bf, res, HALF + LAST_ON_SCALAR, S)
        weave(nc.scalar.copy, res_bf, res, HALF, HALF + LAST_ON_SCALAR)

        for half in range(2):
            cols = half_cols(half)
            nc.vector.quantize_mx(out=res_codes[half][:].bitcast(FP8X4), scales=res_scales[:, cols], in_=res_bf[:, PACK * half * HALF : PACK * (half + 1) * HALF])
            nc.sync.dma_start(out=out_words[:, cols], in_=res_codes[half][:].bitcast(I32))
        for q in range(4):
            queue = nc.scalar if q % 2 == 0 else nc.sync
            queue.dma_start(
                out=out_2[0, 4 * q : 4 * q + 4, :].bitcast(I32), in_=res_scales[32 * q : 32 * q + 4, :].bitcast(I32)
            )
